import numpy as np
import ml_dtypes


def mxq(x, axis, fmt="e4m3"):
    dtype, down = {"e4m3": (ml_dtypes.float8_e4m3fn, 7), "e5m2": (ml_dtypes.float8_e5m2, 14)}[fmt]
    v = np.moveaxis(np.asarray(x, np.float32).astype(ml_dtypes.bfloat16).astype(np.float64), axis, -1)
    blocks = v.reshape(v.shape[:-1] + (-1, 32))
    amax = np.abs(blocks).max(-1, keepdims=True)
    byte = np.maximum(np.where(amax > 0, np.frexp(amax)[1] - 1 + 127, 0) - down, 1)
    scale = np.exp2(byte - 127.0)
    codes = (blocks / scale).astype(np.float32).astype(dtype).astype(np.float64)
    return np.moveaxis((codes * scale).reshape(v.shape), -1, axis)


WIDE = False


def mx_kscale(k):
    if not WIDE:
        return np.ones(k)
    levels = np.array([10, -10, 5, -5, 0])
    if k % 512:
        return np.exp2(np.random.permutation(np.resize(levels, k // 32))).repeat(32)
    a = np.empty((k // 512, 16))
    for p in range(k // 512):
        a[p, :8] = np.random.permutation(np.resize(levels, 8))
        for g in range(8):
            far = levels[np.abs(levels - a[p, g]) >= 10]
            a[p, g + 8] = far[np.random.randint(len(far))]
    return np.exp2(a.ravel()).repeat(32)


def f64(x):
    return np.asarray(x).astype(np.float64)


def striped(idx):
    return np.tile(idx.reshape(-1, 16).T, (8, 1)).astype(np.uint16)


def unstriped(offs):
    return offs[:16].T.reshape(-1).astype(np.int64)


def striped8(idx):
    return np.concatenate([x.reshape(-1, 16).T for x in idx]).astype(np.uint16)


def runs(offs, k):
    lists = np.stack([offs[16 * r : 16 * r + 16].T.reshape(-1) for r in range(8)]).astype(np.int64)
    return lists[np.arange(k) % 512 // 64]


def pack_weight(w):
    k, n = w.shape
    w = f64(np.asarray(w, np.float32).astype(ml_dtypes.bfloat16)).reshape(k // 32, 32, n)
    amax = np.abs(w).max(1)
    byte = np.clip(np.where(amax > 0, np.frexp(amax)[1] - 1 + 127 - 7, 1), 1, 254)
    scaled = (w * np.exp2(127.0 - byte)[:, None, :]).reshape(k, n).astype(np.float32)
    words = np.ascontiguousarray(scaled.reshape(k // 512, 128, 4, n).transpose(0, 1, 3, 2)).astype(ml_dtypes.float8_e4m3fn).view(np.uint8)
    return words, np.ascontiguousarray(byte.astype(np.uint8).reshape(k // 512, 16, n))


def unpack_weight(words, scales):
    g, p, n, _ = words.shape
    vals = np.ascontiguousarray(words).view(ml_dtypes.float8_e4m3fn).astype(np.float64) * np.repeat(np.exp2(scales.astype(np.float64) - 127.0), 8, axis=1)[..., None]
    return vals.transpose(0, 1, 3, 2).reshape(g * 512, n)


K, T, S, N, H = 512, 2048, 512, 512, 512


def setup_inputs():
    n = np.random.standard_normal
    s = mx_kscale(K)[:, None]
    u = mx_kscale(H)
    packed_xT = pack_weight(n((K, T)) * s)
    return {
        "x_words": packed_xT[0],
        "x_scales": packed_xT[1],
        "w1": (n((K, H)) / np.sqrt(K) / s).astype(np.float32),
        "cj1": (0.7 * n((H, S))).astype(np.float32),
        "cj2": (0.7 * n((H, S))).astype(np.float32),
        "gn": (np.random.uniform(0.5, 1.5, (H, 1)) * u[:, None]).astype(np.float32),
        "w2": (n((H, N)) / np.sqrt(H) / u[:, None]).astype(np.float32),
        "offs": striped(np.random.permutation(T)[:S]),
        "p1": striped8(np.stack([np.random.permutation(S) for _ in range(8)])),
        "p2": striped8(np.stack([np.random.permutation(S) for _ in range(8)])),
    }


def reference(x_words, x_scales, w1, cj1, cj2, gn, w2, offs, p1, p2):
    xq = unpack_weight(x_words, x_scales)[:, unstriped(offs)]
    y = mxq(f64(w1), 0, "e4m3").T @ xq
    h = np.tanh(y + f64(cj1) * (y[np.arange(H)[:, None], runs(p1, H)]) + f64(cj2) * (y[np.arange(H)[:, None], runs(p2, H)]))
    z = f64(gn) * (np.tanh(y + f64(cj1) * (h[np.arange(H)[:, None], runs(p1, H)]) + f64(cj2) * (h[np.arange(H)[:, None], runs(p2, H)])))
    return mxq(f64(w2), 0, "e4m3").T @ mxq(z, 0, "e4m3")

@@ -1,0 +1,207 @@
+from contextlib import ExitStack
+
+import concourse.mybir as mybir
+from concourse.masks import make_identity
+
+K, T, S, H, N = 512, 2048, 512, 512, 512
+FLOPS = 2 * K * H * S + 2 * H * N * S
+
+F32 = mybir.dt.float32
+BF16 = mybir.dt.bfloat16
+I32 = mybir.dt.int32
+U32 = mybir.dt.uint32
+U16 = mybir.dt.uint16
+U8 = mybir.dt.uint8
+FP8X4 = mybir.dt.float8_e4m3fn_x4
+ACT = mybir.ActivationFunctionType
+ALU = mybir.AluOpType
+
+P = 128
+PACK = 4
+HALF = S // 2
+W1_VECTOR_M = 88
+
+
+def tile_picked_mfield_none_p_kernel(
+    tc, x_words, x_scales, w1, cj1, cj2, gn, w2, offs, p1, p2, out
+):
+    nc = tc.nc
+    with ExitStack() as ctx:
+        keep = ctx.enter_context(tc.tile_pool(name="keep", bufs=1))
+        psum = ctx.enter_context(tc.psum_pool(name="psum", bufs=1))
+
+        def sb(shape, dtype, name):
+            return keep.tile(shape, dtype, name=name, align_bytes=64)
+
+        def bank(tag, name):
+            return psum.tile([P, 512], F32, name=name, tag=tag)
+
+        offs_t = sb([P, S // 16], U16, "offs_t")
+        p1_t = sb([P, S // 16], U16, "p1_t")
+        p2_t = sb([P, S // 16], U16, "p2_t")
+        lists = (p1_t, p2_t)
+
+        xs_win = sb([P, T], U8, "xs_win")
+        xw_win = sb([P, T], I32, "xw_win")
+        w1_raw = sb([P, PACK, H], F32, "w1_raw")
+        w2_raw = sb([P, PACK, N], F32, "w2_raw")
+        gn_t = sb([P, PACK], F32, "gn_t")
+        cj = [[sb([P, S], F32, f"cj{n}_{t}") for n in range(2)] for t in range(PACK)]
+        y_win = [sb([P, 2 * S], F32, f"y_win{t}") for t in range(PACK)]
+        ident = sb([P, P], F32, "ident")
+
+        nc.vector.memset(xs_win[:].bitcast(I32), 0)
+        for q in range(4):
+            nc.scalar.dma_start(
+                out=xs_win[32 * q : 32 * q + 4, :].bitcast(I32),
+                in_=x_scales[0, 4 * q : 4 * q + 4, :].bitcast(I32),
+            )
+        nc.sync.dma_start(out=offs_t[:], in_=offs)
+        nc.sync.dma_start(out=w1_raw[:], in_=w1.rearrange("(p j) c -> p j c", j=PACK))
+        nc.sync.dma_start(out=xw_win[:], in_=x_words[0].rearrange("p n r -> p (n r)").bitcast(I32))
+        nc.sync.dma_start(out=p1_t[:], in_=p1)
+        nc.sync.dma_start(out=p2_t[:], in_=p2)
+        cj_rows = [c.rearrange("(p t) j -> p t j", t=PACK) for c in (cj1, cj2)]
+        for t in range(PACK):
+            for n in range(2):
+                nc.sync.dma_start(out=cj[t][n][:], in_=cj_rows[n][:, t, :])
+            if t == 1:
+                nc.sync.dma_start(out=w2_raw[:], in_=w2.rearrange("(p j) c -> p j c", j=PACK))
+        nc.sync.dma_start(out=gn_t[:], in_=gn.rearrange("(p t) o -> p (t o)", t=PACK))
+
+        for t in range(PACK):
+            nc.vector.memset(y_win[t][:, S:], 0.0)
+        make_identity(nc, ident[:])
+
+        xs_pick = sb([P, S], U8, "xs_pick")
+        nc.vector.tensor_copy(out=xs_pick[:], in_=xs_win[:].indirect(offs_t[:]))
+
+        w1_b = sb([P, PACK * H], BF16, "w1_b")
+        w1_dst = w1_b[:].rearrange("p (t m j) -> p m j t", t=PACK, j=PACK)
+        w1_src = w1_raw[:].rearrange("p j (m t) -> p m j t", t=PACK)
+        nc.vector.tensor_copy(out=w1_dst[:, :W1_VECTOR_M], in_=w1_src[:, :W1_VECTOR_M])
+        nc.scalar.copy(out=w1_dst[:, W1_VECTOR_M:], in_=w1_src[:, W1_VECTOR_M:])
+        w1_codes = sb([P, H], U32, "w1_codes")
+        w1_scales = sb([P, H], U8, "w1_scales")
+        nc.vector.quantize_mx(out=w1_codes[:].bitcast(FP8X4), scales=w1_scales[:], in_=w1_b[:])
+
+        xw_pick = sb([P, S], U32, "xw_pick")
+        nc.vector.tensor_copy(out=xw_pick[:], in_=xw_win[:].bitcast(U32).indirect(offs_t[:]))
+
+        for t in range(PACK):
+            cols = slice(t * P, (t + 1) * P)
+            y_bank = bank(f"B{t}", f"y_bank{t}")
+            nc.tensor.matmul_mx(
+                out=y_bank[:],
+                lhsT=w1_codes[:, cols].bitcast(FP8X4),
+                lhsT_scale=w1_scales[:, cols],
+                rhs=xw_pick[:].bitcast(FP8X4),
+                rhs_scale=xs_pick[:],
+                start=True,
+                stop=True,
+            )
+            nc.scalar.activation(out=y_win[t][:, :S], in_=y_bank[:], func=ACT.Copy, scale=0.5)
+
+        sum_banks = [bank(f"U{b}", f"sum_bank{b}") for b in range(4)]
+
+        def add_turned(b, t, src, start=False, stop=False):
+            nc.tensor.matmul(
+                out=sum_banks[b][:, t * P : (t + 1) * P],
+                lhsT=src,
+                rhs=ident[:],
+                start=start,
+                stop=stop,
+                is_transpose=True,
+            )
+
+        for t in range(PACK):
+            for b in range(4):
+                add_turned(b, t, y_win[t][:, b * P : (b + 1) * P], start=(t == 0))
+
+        w2_b = sb([P, PACK * N], BF16, "w2_b")
+        w2_dst = w2_b[:].rearrange("p (c i j) -> p c j i", i=4, j=PACK)
+        w2_src = w2_raw[:].rearrange("p j (c i) -> p c j i", i=4)
+        for hf in range(2):
+            nc.scalar.copy(out=w2_dst[:, 64 * hf : 64 * hf + 64], in_=w2_src[:, 64 * hf : 64 * hf + 64])
+
+        u_win = [sb([P, S], F32, f"u_win{t}") for t in range(PACK)]
+        sig = {}
+        for t in range(PACK):
+            terms = []
+            for n in range(2):
+                term = sb([P, S], F32, f"term{t}_{n}")
+                nc.vector.tensor_tensor(
+                    out=term[:], in0=y_win[t][:].indirect(lists[n][:]), in1=cj[t][n][:], op=ALU.mult
+                )
+                terms.append(term)
+            part = sb([P, S], F32, f"part{t}")
+            nc.vector.tensor_tensor(out=part[:], in0=y_win[t][:, :S], in1=terms[0][:], op=ALU.add)
+            nc.vector.tensor_tensor(out=u_win[t][:], in0=part[:], in1=terms[1][:], op=ALU.add)
+            for hf in range(2):
+                for n in range(2):
+                    s_t = sb([P, HALF], F32, f"sig{t}_{hf}_{n}")
+                    nc.scalar.activation(
+                        out=s_t[:],
+                        in_=u_win[t][:].indirect(lists[n][:, 16 * hf : 16 * hf + 16]),
+                        func=ACT.Sigmoid,
+                        scale=4.0,
+                    )
+                    sig[t, hf, n] = s_t
+
+        for hf in range(2):
+            for t in range(PACK):
+                for n in range(2):
+                    prod = sb([P, HALF], F32, f"prod{t}_{hf}_{n}")
+                    nc.vector.scalar_tensor_tensor(
+                        out=prod[:],
+                        in0=sig[t, hf, n][:],
+                        scalar=-0.5,
+                        in1=cj[t][n][:, hf * HALF : (hf + 1) * HALF],
+                        op0=ALU.add,
+                        op1=ALU.mult,
+                    )
+                    for i in range(2):
+                        add_turned(2 * hf + i, t, prod[:, i * P : (i + 1) * P], stop=(t == PACK - 1 and n == 1))
+
+        w2_codes = sb([P, N], U32, "w2_codes")
+        w2_scales = sb([P, N], U8, "w2_scales")
+        nc.vector.quantize_mx(out=w2_codes[:].bitcast(FP8X4), scales=w2_scales[:], in_=w2_b[:])
+
+        out_rows = out.rearrange("(mb m) j -> m mb j", m=P)
+        z_b = []
+        for b in range(4):
+            th = sb([P, PACK * P], F32, f"th{b}")
+            nc.scalar.activation(out=th[:], in_=sum_banks[b][:], func=ACT.Tanh, scale=2.0)
+            back = bank(f"B{b}", f"back{b}")
+            for t in range(PACK):
+                nc.tensor.transpose(out=back[:, t * P : (t + 1) * P], in_=th[:, t * P : (t + 1) * P], identity=ident[:])
+            z = sb([P, P * PACK], BF16, f"z{b}")
+            nc.vector.tensor_tensor(
+                out=z[:].rearrange("p (j t) -> p j t", t=PACK),
+                in0=back[:].rearrange("p (t j) -> p j t", t=PACK),
+                in1=gn_t[:].unsqueeze(1).to_broadcast([P, P, PACK]),
+                op=ALU.mult,
+            )
+            z_b.append(z)
+        for b in range(4):
+            z_codes = sb([P, P], U32, f"z_codes{b}")
+            z_scales = sb([P, P], U8, f"z_scales{b}")
+            nc.vector.quantize_mx(out=z_codes[:].bitcast(FP8X4), scales=z_scales[:], in_=z_b[b][:])
+            o_bank = bank(f"U{b}", f"o_bank{b}")
+            for mb in range(4):
+                cols = slice(mb * P, (mb + 1) * P)
+                nc.tensor.matmul_mx(
+                    out=o_bank[:, cols],
+                    lhsT=w2_codes[:, cols].bitcast(FP8X4),
+                    lhsT_scale=w2_scales[:, cols],
+                    rhs=z_codes[:].bitcast(FP8X4),
+                    rhs_scale=z_scales[:],
+                    start=True,
+                    stop=True,
+                )
+            o_sb = sb([P, 4, P], F32, f"o_sb{b}")
+            if b == 3:
+                nc.vector.tensor_copy(out=o_sb[:].rearrange("p a j -> p (a j)"), in_=o_bank[:])
+            else:
+                nc.scalar.copy(out=o_sb[:].rearrange("p a j -> p (a j)"), in_=o_bank[:])
+            nc.sync.dma_start(out=out_rows[:, :, b * P : (b + 1) * P], in_=o_sb[:])

@@ -20,6 +20,8 @@ P = 128
 PACK = 4
 HALF = S // 2
 W1_VECTOR_M = 88
+Y_SCALE = (0.5, 0.5, 0.5, 1.0)
+BLOCK_SLOT = {0: 0, 2: 1, 3: 2}
 
 
 def tile_picked_mfield_none_p_kernel(
@@ -41,6 +43,7 @@ def tile_picked_mfield_none_p_kernel(
         p2_t = sb([P, S // 16], U16, "p2_t")
         lists = (p1_t, p2_t)
 
+        xs_rows = sb([P, T], U8, "xs_rows")
         xs_win = sb([P, T], U8, "xs_win")
         xw_win = sb([P, T], I32, "xw_win")
         w1_raw = sb([P, PACK, H], F32, "w1_raw")
@@ -52,8 +55,8 @@ def tile_picked_mfield_none_p_kernel(
 
         nc.vector.memset(xs_win[:].bitcast(I32), 0)
         for q in range(4):
-            nc.scalar.dma_start(
-                out=xs_win[32 * q : 32 * q + 4, :].bitcast(I32),
+            nc.sync.dma_start(
+                out=xs_rows[32 * q : 32 * q + 4, :].bitcast(I32),
                 in_=x_scales[0, 4 * q : 4 * q + 4, :].bitcast(I32),
             )
         nc.sync.dma_start(out=offs_t[:], in_=offs)
@@ -65,14 +68,19 @@ def tile_picked_mfield_none_p_kernel(
         for t in range(PACK):
             for n in range(2):
                 nc.sync.dma_start(out=cj[t][n][:], in_=cj_rows[n][:, t, :])
-            if t == 1:
+            if t == 0:
                 nc.sync.dma_start(out=w2_raw[:], in_=w2.rearrange("(p j) c -> p j c", j=PACK))
         nc.sync.dma_start(out=gn_t[:], in_=gn.rearrange("(p t) o -> p (t o)", t=PACK))
 
         for t in range(PACK):
             nc.vector.memset(y_win[t][:, S:], 0.0)
         make_identity(nc, ident[:])
+        warm = sb([P, 1], F32, "warm")
+        nc.scalar.activation(out=warm[:], in_=y_win[0][:, S : S + 1], func=ACT.Sigmoid)
 
+        for q in range(4):
+            rows = slice(32 * q, 32 * q + 4)
+            nc.vector.tensor_copy(out=xs_win[rows, :].bitcast(I32), in_=xs_rows[rows, :].bitcast(I32))
         xs_pick = sb([P, S], U8, "xs_pick")
         nc.vector.tensor_copy(out=xs_pick[:], in_=xs_win[:].indirect(offs_t[:]))
 
@@ -86,37 +94,168 @@ def tile_picked_mfield_none_p_kernel(
         nc.vector.quantize_mx(out=w1_codes[:].bitcast(FP8X4), scales=w1_scales[:], in_=w1_b[:])
 
         xw_pick = sb([P, S], U32, "xw_pick")
-        nc.vector.tensor_copy(out=xw_pick[:], in_=xw_win[:].bitcast(U32).indirect(offs_t[:]))
+        for hf in range(2):
+            nc.vector.tensor_copy(
+                out=xw_pick[:, hf * HALF : (hf + 1) * HALF],
+                in_=xw_win[:].bitcast(U32).indirect(offs_t[:, 16 * hf : 16 * hf + 16]),
+            )
 
-        for t in range(PACK):
+        def field(t, lo, hi, tag):
             cols = slice(t * P, (t + 1) * P)
-            y_bank = bank(f"B{t}", f"y_bank{t}")
+            y_bank = bank(tag, f"y_bank{t}_{lo}")
             nc.tensor.matmul_mx(
-                out=y_bank[:],
+                out=y_bank[:, : hi - lo],
                 lhsT=w1_codes[:, cols].bitcast(FP8X4),
                 lhsT_scale=w1_scales[:, cols],
-                rhs=xw_pick[:].bitcast(FP8X4),
-                rhs_scale=xs_pick[:],
+                rhs=xw_pick[:, lo:hi].bitcast(FP8X4),
+                rhs_scale=xs_pick[:, lo:hi],
                 start=True,
                 stop=True,
             )
-            nc.scalar.activation(out=y_win[t][:, :S], in_=y_bank[:], func=ACT.Copy, scale=0.5)
+            nc.scalar.activation(out=y_win[t][:, lo:hi], in_=y_bank[:, : hi - lo], func=ACT.Copy, scale=Y_SCALE[t])
 
-        sum_banks = [bank(f"U{b}", f"sum_bank{b}") for b in range(4)]
+        field(0, 0, HALF, "U3")
+        field(0, HALF, S, "B0")
+        for t in range(1, PACK):
+            field(t, 0, S, f"B{t}")
 
-        def add_turned(b, t, src, start=False, stop=False):
+        sums, sig, terms, part, z_b = {}, {}, {}, {}, {}
+        u_win = [sb([P, 2 * S if t == 1 else S], F32, f"u_win{t}") for t in range(PACK)]
+        for t in range(PACK):
+            part[t] = sb([P, S], F32, f"part{t}")[:]
+        sig0 = w2_raw[:].rearrange("p j c -> p (j c)")[:, P : P + 2 * S]
+
+        def turn_into(acc, lo, b, src, start=False, stop=False):
             nc.tensor.matmul(
-                out=sum_banks[b][:, t * P : (t + 1) * P],
-                lhsT=src,
-                rhs=ident[:],
-                start=start,
-                stop=stop,
-                is_transpose=True,
+                out=acc[:, b * P - lo : (b + 1) * P - lo], lhsT=src, rhs=ident[:], start=start, stop=stop, is_transpose=True
             )
 
-        for t in range(PACK):
+        def open_sum(t, lo, hi, tag, key=None):
+            key = t if key is None else key
+            sums[key, lo] = bank(tag, f"sum{key}_{lo}")
+            for b in range(lo // P, hi // P):
+                turn_into(sums[key, lo], lo, b, y_win[t][:, b * P : (b + 1) * P], start=(b * P == lo))
+
+        def gather1(t, n, key=None):
+            if t == 3:
+                terms[t, n] = sig0[:, n * S : (n + 1) * S]
+            elif (t, n) == (1, 1):
+                terms[t, n] = u_win[1][:, S:]
+            else:
+                terms[t, n] = sb([P, S], F32, f"term{t}_{n}")[:]
+            nc.vector.tensor_tensor(
+                out=terms[t, n], in0=y_win[t][:].indirect(lists[n][:]), in1=cj[t][n][:], op=ALU.mult
+            )
+            if key is not None:
+                for b in range(4):
+                    turn_into(sums[key, 0], 0, b, terms[t, n][:, b * P : (b + 1) * P], stop=(n == 1 and b == 3))
+
+        def sum_out(t, key):
+            nc.scalar.copy(out=part[t], in_=sums[key, 0][:])
+
+        def sum_back(t, tag):
+            turned = bank(tag, f"turned{t}")
             for b in range(4):
-                add_turned(b, t, y_win[t][:, b * P : (b + 1) * P], start=(t == 0))
+                nc.tensor.transpose(out=turned[:, b * P : (b + 1) * P], in_=part[t][:, b * P : (b + 1) * P], identity=ident[:])
+            nc.scalar.copy(out=u_win[t][:, :S], in_=turned[:])
+
+        def add_first(t):
+            nc.vector.tensor_tensor(out=part[t], in0=y_win[t][:, :S], in1=terms[t, 0], op=ALU.add)
+
+        def add_second(t):
+            nc.vector.tensor_tensor(out=u_win[t][:, :S], in0=part[t], in1=terms[t, 1], op=ALU.add)
+
+        def gather2(t, lo, hi):
+            for n in range(2):
+                if t == 2:
+                    sig[t, lo, n] = u_win[1][:, 2 * lo + n * HALF : 2 * lo + (n + 1) * HALF]
+                elif t == 0:
+                    sig[t, lo, n] = sig0[:, 2 * lo + n * HALF : 2 * lo + (n + 1) * HALF]
+                else:
+                    sig[t, lo, n] = sb([P, hi - lo], F32, f"sig{t}_{lo}_{n}")[:]
+                nc.scalar.activation(
+                    out=sig[t, lo, n],
+                    in_=u_win[t][:].indirect(lists[n][:, lo // 16 : hi // 16]),
+                    func=ACT.Sigmoid,
+                    scale=4.0,
+                )
+
+        def products(t, lo, hi, sum_lo, last):
+            for n in range(2):
+                if (t, lo) == (0, 0):
+                    prod = part[1][:, n * HALF : (n + 1) * HALF]
+                else:
+                    prod = sb([P, hi - lo], F32, f"prod{t}_{lo}_{n}")[:]
+                nc.vector.scalar_tensor_tensor(
+                    out=prod, in0=sig[t, lo, n], scalar=-0.5, in1=cj[t][n][:, lo:hi], op0=ALU.add, op1=ALU.mult
+                )
+                for b in range(lo // P, hi // P):
+                    turn_into(
+                        sums[t, sum_lo], sum_lo, b, prod[:, b * P - lo : (b + 1) * P - lo],
+                        stop=(last and n == 1 and (b + 1) * P == hi),
+                    )
+
+        h_win = u_win[2]
+
+        def gather_products(t, lo, hi):
+            for n in range(2):
+                prod = sb([P, hi - lo], F32, f"prod{t}_{lo}_{n}")
+                nc.vector.tensor_tensor(
+                    out=prod[:], in0=h_win[:].indirect(lists[n][:, lo // 16 : hi // 16]), in1=cj[t][n][:, lo:hi], op=ALU.mult
+                )
+                turn_into(sums[t, lo], lo, lo // P, prod[:], stop=(n == 1))
+
+        def tanh_and_back(t, lo, hi, scale=2.0):
+            th = sb([P, hi - lo], F32, f"th{t}_{lo}")
+            nc.scalar.activation(out=th[:], in_=sums[t, lo][:, : hi - lo], func=ACT.Tanh, scale=scale)
+            for b in range(lo // P, hi // P):
+                nc.tensor.transpose(
+                    out=backs[b][:, t * P : (t + 1) * P], in_=th[:, b * P - lo : (b + 1) * P - lo], identity=ident[:]
+                )
+
+        def gain(b):
+            z_b[b] = sb([P, P * PACK], BF16, f"z{b}")
+            nc.vector.tensor_tensor(
+                out=z_b[b][:].rearrange("p (j t) -> p j t", t=PACK),
+                in0=backs[b][:].rearrange("p (t j) -> p j t", t=PACK),
+                in1=gn_t[:].unsqueeze(1).to_broadcast([P, P, PACK]),
+                op=ALU.mult,
+            )
+
+        w2_codes = sb([P, N], U32, "w2_codes")
+        w2_scales = sb([P, N], U8, "w2_scales")
+        out_rows = out.rearrange("(mb m) j -> m mb j", m=P)
+
+        def layer(b, tags):
+            z_codes = sb([P, P], U32, f"z_codes{b}")
+            z_scales = sb([P, P], U8, f"z_scales{b}")
+            nc.vector.quantize_mx(out=z_codes[:].bitcast(FP8X4), scales=z_scales[:], in_=z_b[b][:])
+            per = 4 // len(tags)
+            for g, tag in enumerate(tags):
+                o_bank = bank(tag, f"o_bank{b}_{g}")
+                for i in range(per):
+                    cols = slice((g * per + i) * P, (g * per + i + 1) * P)
+                    nc.tensor.matmul_mx(
+                        out=o_bank[:, i * P : (i + 1) * P],
+                        lhsT=w2_codes[:, cols].bitcast(FP8X4),
+                        lhsT_scale=w2_scales[:, cols],
+                        rhs=z_codes[:].bitcast(FP8X4),
+                        rhs_scale=z_scales[:],
+                        start=True,
+                        stop=True,
+                    )
+                o_sb = sb([P, per, P], F32, f"o_sb{b}_{g}")
+                if g == 1:
+                    nc.vector.tensor_copy(out=o_sb[:].rearrange("p a j -> p (a j)"), in_=o_bank[:, : per * P])
+                else:
+                    nc.scalar.copy(out=o_sb[:].rearrange("p a j -> p (a j)"), in_=o_bank[:, : per * P])
+                nc.sync.dma_start(out=out_rows[:, g * per : (g + 1) * per, b * P : (b + 1) * P], in_=o_sb[:])
+
+        open_sum(1, 0, S, "B1", "r1")
+        open_sum(0, 0, S, "U0")
+        open_sum(1, 0, S, "U1")
+        open_sum(2, 0, HALF, "U2")
+        open_sum(2, HALF, S, "U3")
 
         w2_b = sb([P, PACK * N], BF16, "w2_b")
         w2_dst = w2_b[:].rearrange("p (c i j) -> p c j i", i=4, j=PACK)
@@ -124,84 +263,58 @@ def tile_picked_mfield_none_p_kernel(
         for hf in range(2):
             nc.scalar.copy(out=w2_dst[:, 64 * hf : 64 * hf + 64], in_=w2_src[:, 64 * hf : 64 * hf + 64])
 
-        u_win = [sb([P, S], F32, f"u_win{t}") for t in range(PACK)]
-        sig = {}
-        for t in range(PACK):
-            terms = []
-            for n in range(2):
-                term = sb([P, S], F32, f"term{t}_{n}")
-                nc.vector.tensor_tensor(
-                    out=term[:], in0=y_win[t][:].indirect(lists[n][:]), in1=cj[t][n][:], op=ALU.mult
-                )
-                terms.append(term)
-            part = sb([P, S], F32, f"part{t}")
-            nc.vector.tensor_tensor(out=part[:], in0=y_win[t][:, :S], in1=terms[0][:], op=ALU.add)
-            nc.vector.tensor_tensor(out=u_win[t][:], in0=part[:], in1=terms[1][:], op=ALU.add)
-            for hf in range(2):
-                for n in range(2):
-                    s_t = sb([P, HALF], F32, f"sig{t}_{hf}_{n}")
-                    nc.scalar.activation(
-                        out=s_t[:],
-                        in_=u_win[t][:].indirect(lists[n][:, 16 * hf : 16 * hf + 16]),
-                        func=ACT.Sigmoid,
-                        scale=4.0,
-                    )
-                    sig[t, hf, n] = s_t
-
-        for hf in range(2):
-            for t in range(PACK):
-                for n in range(2):
-                    prod = sb([P, HALF], F32, f"prod{t}_{hf}_{n}")
-                    nc.vector.scalar_tensor_tensor(
-                        out=prod[:],
-                        in0=sig[t, hf, n][:],
-                        scalar=-0.5,
-                        in1=cj[t][n][:, hf * HALF : (hf + 1) * HALF],
-                        op0=ALU.add,
-                        op1=ALU.mult,
-                    )
-                    for i in range(2):
-                        add_turned(2 * hf + i, t, prod[:, i * P : (i + 1) * P], stop=(t == PACK - 1 and n == 1))
-
-        w2_codes = sb([P, N], U32, "w2_codes")
-        w2_scales = sb([P, N], U8, "w2_scales")
+        gather1(0, 0)
+        gather1(0, 1)
+        add_first(0)
+        gather1(1, 0, "r1")
+        add_second(0)
+        gather2(0, 0, HALF)
+        gather2(0, HALF, S)
+        gather1(1, 1, "r1")
+        sum_out(1, "r1")
+        sum_back(1, "B2")
+        backs = [bank(f"B{b}", f"back{b}") for b in range(4)]
+        gather1(2, 0)
+        gather1(2, 1)
+        add_first(2)
+        gather2(1, 0, HALF)
+        products(0, 0, HALF, 0, False)
+        add_second(2)
+        products(0, HALF, S, 0, True)
+        gather2(1, HALF, S)
+        tanh_and_back(0, 0, S)
+        open_sum(3, 0, P, "U0")
+        gather1(3, 0)
+        gather2(2, 0, HALF)
+        gather1(3, 1)
+        products(1, 0, HALF, 0, False)
+        add_first(3)
+        gather2(2, HALF, S)
+        products(1, HALF, S, 0, True)
+        add_second(3)
+        nc.scalar.activation(out=h_win[:], in_=u_win[3][:], func=ACT.Tanh)
+        products(2, 0, HALF, 0, True)
+        tanh_and_back(1, 0, S)
+        open_sum(3, P, 2 * P, "U1")
+        products(2, HALF, S, HALF, True)
+        gather_products(3, 0, P)
+        tanh_and_back(2, 0, HALF)
+        open_sum(3, 2 * P, 3 * P, "U2")
+        gather_products(3, P, 2 * P)
+        tanh_and_back(3, 0, P, 1.0)
+        tanh_and_back(2, HALF, S)
+        open_sum(3, 3 * P, S, "U3")
+        gather_products(3, 2 * P, 3 * P)
+        tanh_and_back(3, P, 2 * P, 1.0)
+        gather_products(3, 3 * P, S)
         nc.vector.quantize_mx(out=w2_codes[:].bitcast(FP8X4), scales=w2_scales[:], in_=w2_b[:])
-
-        out_rows = out.rearrange("(mb m) j -> m mb j", m=P)
-        z_b = []
-        for b in range(4):
-            th = sb([P, PACK * P], F32, f"th{b}")
-            nc.scalar.activation(out=th[:], in_=sum_banks[b][:], func=ACT.Tanh, scale=2.0)
-            back = bank(f"B{b}", f"back{b}")
-            for t in range(PACK):
-                nc.tensor.transpose(out=back[:, t * P : (t + 1) * P], in_=th[:, t * P : (t + 1) * P], identity=ident[:])
-            z = sb([P, P * PACK], BF16, f"z{b}")
-            nc.vector.tensor_tensor(
-                out=z[:].rearrange("p (j t) -> p j t", t=PACK),
-                in0=back[:].rearrange("p (t j) -> p j t", t=PACK),
-                in1=gn_t[:].unsqueeze(1).to_broadcast([P, P, PACK]),
-                op=ALU.mult,
-            )
-            z_b.append(z)
-        for b in range(4):
-            z_codes = sb([P, P], U32, f"z_codes{b}")
-            z_scales = sb([P, P], U8, f"z_scales{b}")
-            nc.vector.quantize_mx(out=z_codes[:].bitcast(FP8X4), scales=z_scales[:], in_=z_b[b][:])
-            o_bank = bank(f"U{b}", f"o_bank{b}")
-            for mb in range(4):
-                cols = slice(mb * P, (mb + 1) * P)
-                nc.tensor.matmul_mx(
-                    out=o_bank[:, cols],
-                    lhsT=w2_codes[:, cols].bitcast(FP8X4),
-                    lhsT_scale=w2_scales[:, cols],
-                    rhs=z_codes[:].bitcast(FP8X4),
-                    rhs_scale=z_scales[:],
-                    start=True,
-                    stop=True,
-                )
-            o_sb = sb([P, 4, P], F32, f"o_sb{b}")
-            if b == 3:
-                nc.vector.tensor_copy(out=o_sb[:].rearrange("p a j -> p (a j)"), in_=o_bank[:])
-            else:
-                nc.scalar.copy(out=o_sb[:].rearrange("p a j -> p (a j)"), in_=o_bank[:])
-            nc.sync.dma_start(out=out_rows[:, :, b * P : (b + 1) * P], in_=o_sb[:])
+        tanh_and_back(3, 2 * P, 3 * P, 1.0)
+        tanh_and_back(3, 3 * P, S, 1.0)
+        gain(0)
+        gain(1)
+        layer(0, ["U0"])
+        gain(2)
+        layer(1, ["U1"])
+        layer(2, ["U2"])
+        gain(3)
+        layer(3, ["U3", "B0"])

@@ -20,8 +20,6 @@ P = 128
 PACK = 4
 HALF = S // 2
 W1_VECTOR_M = 88
-Y_SCALE = (0.5, 0.5, 0.5, 1.0)
-BLOCK_SLOT = {0: 0, 2: 1, 3: 2}
 
 
 def tile_picked_mfield_none_p_kernel(
@@ -47,7 +45,7 @@ def tile_picked_mfield_none_p_kernel(
         xs_win = sb([P, T], U8, "xs_win")
         xw_win = sb([P, T], I32, "xw_win")
         w1_raw = sb([P, PACK, H], F32, "w1_raw")
-        w2_raw = sb([P, PACK, N], F32, "w2_raw")
+        w2_raw = [sb([P, PACK, N // 2], F32, f"w2_raw{h}") for h in range(2)]
         gn_t = sb([P, PACK], F32, "gn_t")
         cj = [[sb([P, S], F32, f"cj{n}_{t}") for n in range(2)] for t in range(PACK)]
         y_win = [sb([P, 2 * S], F32, f"y_win{t}") for t in range(PACK)]
@@ -64,12 +62,13 @@ def tile_picked_mfield_none_p_kernel(
         nc.sync.dma_start(out=xw_win[:], in_=x_words[0].rearrange("p n r -> p (n r)").bitcast(I32))
         nc.sync.dma_start(out=p1_t[:], in_=p1)
         nc.sync.dma_start(out=p2_t[:], in_=p2)
+        w2_rows = w2.rearrange("(p j) c -> p j c", j=PACK)
         cj_rows = [c.rearrange("(p t) j -> p t j", t=PACK) for c in (cj1, cj2)]
         for t in range(PACK):
             for n in range(2):
                 nc.sync.dma_start(out=cj[t][n][:], in_=cj_rows[n][:, t, :])
-            if t == 0:
-                nc.sync.dma_start(out=w2_raw[:], in_=w2.rearrange("(p j) c -> p j c", j=PACK))
+                if t < 2 and n == 0:
+                    nc.sync.dma_start(out=w2_raw[t][:], in_=w2_rows[:, :, t * HALF : (t + 1) * HALF])
         nc.sync.dma_start(out=gn_t[:], in_=gn.rearrange("(p t) o -> p (t o)", t=PACK))
 
         for t in range(PACK):
@@ -112,209 +111,299 @@ def tile_picked_mfield_none_p_kernel(
                 start=True,
                 stop=True,
             )
-            nc.scalar.activation(out=y_win[t][:, lo:hi], in_=y_bank[:, : hi - lo], func=ACT.Copy, scale=Y_SCALE[t])
+            nc.scalar.activation(out=y_win[t][:, lo:hi], in_=y_bank[:, : hi - lo], func=ACT.Copy, scale=0.5)
 
         field(0, 0, HALF, "U3")
         field(0, HALF, S, "B0")
         for t in range(1, PACK):
             field(t, 0, S, f"B{t}")
 
-        sums, sig, terms, part, z_b = {}, {}, {}, {}, {}
-        u_win = [sb([P, 2 * S if t == 1 else S], F32, f"u_win{t}") for t in range(PACK)]
-        for t in range(PACK):
-            part[t] = sb([P, S], F32, f"part{t}")[:]
-        sig0 = w2_raw[:].rearrange("p j c -> p (j c)")[:, P : P + 2 * S]
+        terms, part, r1_sum, sums, sig, z_b, win2 = {}, {}, {}, {}, {}, {}, {}
 
-        def turn_into(acc, lo, b, src, start=False, stop=False):
-            nc.tensor.matmul(
-                out=acc[:, b * P - lo : (b + 1) * P - lo], lhsT=src, rhs=ident[:], start=start, stop=stop, is_transpose=True
-            )
+        def blk(b):
+            return slice(b * P, (b + 1) * P)
 
-        def open_sum(t, lo, hi, tag, key=None):
-            key = t if key is None else key
-            sums[key, lo] = bank(tag, f"sum{key}_{lo}")
-            for b in range(lo // P, hi // P):
-                turn_into(sums[key, lo], lo, b, y_win[t][:, b * P : (b + 1) * P], start=(b * P == lo))
+        def turn_into(acc, slot, src, start=False, stop=False):
+            nc.tensor.matmul(out=acc[:, blk(slot)], lhsT=src, rhs=ident[:], start=start, stop=stop, is_transpose=True)
 
-        def gather1(t, n, key=None):
-            if t == 3:
-                terms[t, n] = sig0[:, n * S : (n + 1) * S]
-            elif (t, n) == (1, 1):
-                terms[t, n] = u_win[1][:, S:]
-            else:
-                terms[t, n] = sb([P, S], F32, f"term{t}_{n}")[:]
+        def open_r1(t, tag):
+            r1_sum[t] = bank(tag, f"r1_sum{t}")
+            for b in range(4):
+                turn_into(r1_sum[t], b, y_win[t][:, blk(b)], start=(b == 0))
+
+        def gather1(t, n, into=None):
+            terms[t, n] = sb([P, S], F32, f"term{t}_{n}")[:] if into is None else into
             nc.vector.tensor_tensor(
                 out=terms[t, n], in0=y_win[t][:].indirect(lists[n][:]), in1=cj[t][n][:], op=ALU.mult
             )
-            if key is not None:
-                for b in range(4):
-                    turn_into(sums[key, 0], 0, b, terms[t, n][:, b * P : (b + 1) * P], stop=(n == 1 and b == 3))
 
-        def sum_out(t, key):
-            nc.scalar.copy(out=part[t], in_=sums[key, 0][:])
-
-        def sum_back(t, tag):
-            turned = bank(tag, f"turned{t}")
+        def add_r1(t, n):
             for b in range(4):
-                nc.tensor.transpose(out=turned[:, b * P : (b + 1) * P], in_=part[t][:, b * P : (b + 1) * P], identity=ident[:])
-            nc.scalar.copy(out=u_win[t][:, :S], in_=turned[:])
+                turn_into(r1_sum[t], b, terms[t, n][:, blk(b)], stop=(n == 1 and b == 3))
 
-        def add_first(t):
+        def add_first(t, into=None):
+            part[t] = sb([P, S], F32, f"part{t}")[:] if into is None else into
             nc.vector.tensor_tensor(out=part[t], in0=y_win[t][:, :S], in1=terms[t, 0], op=ALU.add)
 
-        def add_second(t):
-            nc.vector.tensor_tensor(out=u_win[t][:, :S], in0=part[t], in1=terms[t, 1], op=ALU.add)
+        def add_second(t, tag=None):
+            win2[t] = keep.tile([P, S], F32, name=f"win2_{t}", tag=tag or f"win2_{t}", align_bytes=64)
+            nc.vector.tensor_tensor(out=win2[t][:], in0=part[t], in1=terms[t, 1], op=ALU.add)
 
-        def gather2(t, lo, hi):
-            for n in range(2):
-                if t == 2:
-                    sig[t, lo, n] = u_win[1][:, 2 * lo + n * HALF : 2 * lo + (n + 1) * HALF]
-                elif t == 0:
-                    sig[t, lo, n] = sig0[:, 2 * lo + n * HALF : 2 * lo + (n + 1) * HALF]
-                else:
-                    sig[t, lo, n] = sb([P, hi - lo], F32, f"sig{t}_{lo}_{n}")[:]
-                nc.scalar.activation(
-                    out=sig[t, lo, n],
-                    in_=u_win[t][:].indirect(lists[n][:, lo // 16 : hi // 16]),
-                    func=ACT.Sigmoid,
-                    scale=4.0,
-                )
+        def r1_out(t, with_tanh, into=None):
+            part[t] = sb([P, S], F32, f"part{t}")[:] if into is None else into
+            if into is None:
+                part[t] = part[t].rearrange("p (b j) -> p b j", j=P)
+            nc.scalar.copy(out=part[t], in_=r1_sum[t][:].rearrange("p (b j) -> p b j", j=P))
 
-        def products(t, lo, hi, sum_lo, last):
-            for n in range(2):
-                if (t, lo) == (0, 0):
-                    prod = part[1][:, n * HALF : (n + 1) * HALF]
-                else:
-                    prod = sb([P, hi - lo], F32, f"prod{t}_{lo}_{n}")[:]
-                nc.vector.scalar_tensor_tensor(
-                    out=prod, in0=sig[t, lo, n], scalar=-0.5, in1=cj[t][n][:, lo:hi], op0=ALU.add, op1=ALU.mult
-                )
-                for b in range(lo // P, hi // P):
-                    turn_into(
-                        sums[t, sum_lo], sum_lo, b, prod[:, b * P - lo : (b + 1) * P - lo],
-                        stop=(last and n == 1 and (b + 1) * P == hi),
-                    )
+        def r1_turn(t, bank_tag):
+            turned[t] = bank(bank_tag, f"turned{t}")
+            for b in range(4):
+                nc.tensor.transpose(out=turned[t][:, blk(b)], in_=part[t][:, b, :], identity=ident[:])
 
-        h_win = u_win[2]
+        def r1_back(t, tag=None):
+            win2[t] = keep.tile([P, S], F32, name=f"win2_{t}", tag=tag or f"win2_{t}", align_bytes=64)
+            nc.scalar.copy(out=win2[t][:], in_=turned[t][:])
 
-        def gather_products(t, lo, hi):
-            for n in range(2):
-                prod = sb([P, hi - lo], F32, f"prod{t}_{lo}_{n}")
-                nc.vector.tensor_tensor(
-                    out=prod[:], in0=h_win[:].indirect(lists[n][:, lo // 16 : hi // 16]), in1=cj[t][n][:, lo:hi], op=ALU.mult
-                )
-                turn_into(sums[t, lo], lo, lo // P, prod[:], stop=(n == 1))
+        where, left, whole, h_win, turned, prods, ths = {}, {}, set(), {}, {}, {}, {}
 
-        def tanh_and_back(t, lo, hi, scale=2.0):
-            th = sb([P, hi - lo], F32, f"th{t}_{lo}")
-            nc.scalar.activation(out=th[:], in_=sums[t, lo][:, : hi - lo], func=ACT.Tanh, scale=scale)
+        def open_r2(key, pieces, tag, full=()):
+            sums[key] = bank(tag, f"sum_{key}")
+            left[key] = 2 * len(pieces)
+            for slot, (t, b) in enumerate(pieces):
+                where[t, b] = (key, slot)
+                turn_into(sums[key], slot, y_win[t][:, blk(b)], start=(slot == 0))
+                if (t, b) in full:
+                    whole.add((t, b))
+                    turn_into(sums[key], slot, y_win[t][:, blk(b)])
+
+        def tanh_window(t, tag=None):
+            h_win[t] = keep.tile([P, S], F32, name=f"h_win{t}", tag=tag or f"h_win{t}", align_bytes=64)
+            nc.scalar.activation(out=h_win[t][:], in_=win2[t][:], func=ACT.Tanh, scale=2.0)
+
+        def add_term(t, b, src):
+            key, slot = where[t, b]
+            left[key] = left[key] - 1
+            turn_into(sums[key], slot, src, stop=(left[key] == 0))
+
+        def gather2(t, n, lo, hi, into=None):
+            sig[t, n, lo] = sb([P, hi - lo], F32, f"sig{t}_{n}_{lo}")[:] if into is None else into
+            nc.scalar.activation(
+                out=sig[t, n, lo],
+                in_=win2[t][:].indirect(lists[n][:, lo // 16 : hi // 16]),
+                func=ACT.Sigmoid,
+                scale=4.0,
+            )
+
+        def product(t, n, lo, hi, into=None):
+            prod = sb([P, hi - lo], F32, f"prod{t}_{n}_{lo}")[:] if into is None else into
+            nc.vector.scalar_tensor_tensor(
+                out=prod, in0=sig[t, n, lo], scalar=-0.5, in1=cj[t][n][:, lo:hi], op0=ALU.add, op1=ALU.mult
+            )
             for b in range(lo // P, hi // P):
-                nc.tensor.transpose(
-                    out=backs[b][:, t * P : (t + 1) * P], in_=th[:, b * P - lo : (b + 1) * P - lo], identity=ident[:]
-                )
+                prods[t, n, b] = prod[:, b * P - lo : (b + 1) * P - lo]
 
-        def gain(b):
-            z_b[b] = sb([P, P * PACK], BF16, f"z{b}")
+        def gather_product(t, n, lo, hi, into=None):
+            prod = sb([P, hi - lo], F32, f"gprod{t}_{n}_{lo}")[:] if into is None else into
             nc.vector.tensor_tensor(
-                out=z_b[b][:].rearrange("p (j t) -> p j t", t=PACK),
+                out=prod, in0=h_win.get(t, win2[t])[:].indirect(lists[n][:, lo // 16 : hi // 16]), in1=cj[t][n][:, lo:hi], op=ALU.mult
+            )
+            for b in range(lo // P, hi // P):
+                prods[t, n, b] = prod[:, b * P - lo : (b + 1) * P - lo]
+
+        def add_r2(t, n, blocks):
+            for b in blocks:
+                add_term(t, b, prods[t, n, b])
+
+        def tanh(key, into=None):
+            pieces = sorted([(slot, t, b) for (t, b), (k, slot) in where.items() if k == key])
+            width = len(pieces) * P
+            th = sb([P, width], F32, f"th_{key}")[:] if into is None else into
+            cut = P * len([1 for slot, t, b in pieces if (t, b) in whole])
+            if cut > 0:
+                nc.scalar.activation(out=th[:, :cut], in_=sums[key][:, :cut], func=ACT.Tanh, scale=1.0)
+            if cut < width:
+                nc.scalar.activation(out=th[:, cut:], in_=sums[key][:, cut:width], func=ACT.Tanh, scale=2.0)
+            ths[key] = (th, pieces)
+
+        def back(key):
+            th, pieces = ths[key]
+            for slot, t, b in pieces:
+                nc.tensor.transpose(out=backs[b][:, blk(t)], in_=th[:, blk(slot)], identity=ident[:])
+
+        def gain(b, into=None):
+            z_b[b] = sb([P, P * PACK], BF16, f"z{b}")[:] if into is None else into
+            nc.vector.tensor_tensor(
+                out=z_b[b].rearrange("p (j t) -> p j t", t=PACK),
                 in0=backs[b][:].rearrange("p (t j) -> p j t", t=PACK),
                 in1=gn_t[:].unsqueeze(1).to_broadcast([P, P, PACK]),
                 op=ALU.mult,
             )
 
-        w2_codes = sb([P, N], U32, "w2_codes")
         w2_scales = sb([P, N], U8, "w2_scales")
         out_rows = out.rearrange("(mb m) j -> m mb j", m=P)
 
-        def layer(b, tags):
+        z_q, o_banks = {}, {}
+
+        def quantize_z(b):
             z_codes = sb([P, P], U32, f"z_codes{b}")
             z_scales = sb([P, P], U8, f"z_scales{b}")
-            nc.vector.quantize_mx(out=z_codes[:].bitcast(FP8X4), scales=z_scales[:], in_=z_b[b][:])
-            per = 4 // len(tags)
-            for g, tag in enumerate(tags):
-                o_bank = bank(tag, f"o_bank{b}_{g}")
-                for i in range(per):
-                    cols = slice((g * per + i) * P, (g * per + i + 1) * P)
-                    nc.tensor.matmul_mx(
-                        out=o_bank[:, i * P : (i + 1) * P],
-                        lhsT=w2_codes[:, cols].bitcast(FP8X4),
-                        lhsT_scale=w2_scales[:, cols],
-                        rhs=z_codes[:].bitcast(FP8X4),
-                        rhs_scale=z_scales[:],
-                        start=True,
-                        stop=True,
-                    )
-                o_sb = sb([P, per, P], F32, f"o_sb{b}_{g}")
-                if g == 1:
-                    nc.vector.tensor_copy(out=o_sb[:].rearrange("p a j -> p (a j)"), in_=o_bank[:, : per * P])
-                else:
-                    nc.scalar.copy(out=o_sb[:].rearrange("p a j -> p (a j)"), in_=o_bank[:, : per * P])
-                nc.sync.dma_start(out=out_rows[:, g * per : (g + 1) * per, b * P : (b + 1) * P], in_=o_sb[:])
+            nc.vector.quantize_mx(out=z_codes[:].bitcast(FP8X4), scales=z_scales[:], in_=z_b[b])
+            z_q[b] = (z_codes, z_scales)
 
-        open_sum(1, 0, S, "B1", "r1")
-        open_sum(0, 0, S, "U0")
-        open_sum(1, 0, S, "U1")
-        open_sum(2, 0, HALF, "U2")
-        open_sum(2, HALF, S, "U3")
+        def layer(b, lo, hi, tag):
+            o_banks[b, lo] = bank(tag, f"o_bank{b}_{lo}")
+            for mb in range(lo, hi):
+                nc.tensor.matmul_mx(
+                    out=o_banks[b, lo][:, blk(mb - lo)],
+                    lhsT=w2_q["codes"][:, blk(mb)].bitcast(FP8X4),
+                    lhsT_scale=w2_scales[:, blk(mb)],
+                    rhs=z_q[b][0][:].bitcast(FP8X4),
+                    rhs_scale=z_q[b][1][:],
+                    start=True,
+                    stop=True,
+                )
+
+        def store(b, lo, hi, on_vector=False):
+            o_sb = sb([P, hi - lo, P], F32, f"o_sb{b}_{lo}")
+            src = o_banks[b, lo][:, : (hi - lo) * P]
+            if on_vector:
+                nc.vector.tensor_copy(out=o_sb[:].rearrange("p a j -> p (a j)"), in_=src)
+            else:
+                nc.scalar.copy(out=o_sb[:].rearrange("p a j -> p (a j)"), in_=src)
+            nc.sync.dma_start(out=out_rows[:, lo:hi, blk(b)], in_=o_sb[:])
 
         w2_b = sb([P, PACK * N], BF16, "w2_b")
         w2_dst = w2_b[:].rearrange("p (c i j) -> p c j i", i=4, j=PACK)
-        w2_src = w2_raw[:].rearrange("p j (c i) -> p c j i", i=4)
-        for hf in range(2):
-            nc.scalar.copy(out=w2_dst[:, 64 * hf : 64 * hf + 64], in_=w2_src[:, 64 * hf : 64 * hf + 64])
+        w2_src = [raw[:].rearrange("p j (c i) -> p c j i", i=4) for raw in w2_raw]
 
+        def round_w2(lo, hi):
+            nc.scalar.copy(out=w2_dst[:, lo:hi], in_=w2_src[lo // 64][:, lo % 64 : lo % 64 + hi - lo])
+
+        w2_q = {}
+
+        def quantize_w2(tag="w2_codes"):
+            w2_codes = keep.tile([P, N], U32, name="w2_codes", tag=tag, align_bytes=64)
+            w2_q["codes"] = w2_codes
+            nc.vector.quantize_mx(out=w2_codes[:].bitcast(FP8X4), scales=w2_scales[:], in_=w2_b[:])
+
+        ALL = range(4)
+        open_r1(0, "B0")
+        open_r1(1, "B1")
+        open_r2("t1", [(1, b) for b in ALL], "U1")
+        open_r2("b0", [(2, 0), (3, 0)], "U2", full=[(2, 0)])
+        round_w2(0, 32)
+        round_w2(32, 64)
         gather1(0, 0)
+        add_r1(0, 0)
         gather1(0, 1)
-        add_first(0)
-        gather1(1, 0, "r1")
-        add_second(0)
-        gather2(0, 0, HALF)
-        gather2(0, HALF, S)
-        gather1(1, 1, "r1")
-        sum_out(1, "r1")
-        sum_back(1, "B2")
-        backs = [bank(f"B{b}", f"back{b}") for b in range(4)]
+        add_r1(0, 1)
+        r1_out(0, False)
+        round_w2(64, 96)
+        round_w2(96, 128)
+        gather1(1, 0)
+        add_r1(1, 0)
+        r1_turn(0, "U0")
+        gather1(1, 1)
+        add_r1(1, 1)
+        r1_back(0)
+        r1_out(1, False)
+        r1_turn(1, "U3")
+        open_r2("b2", [(2, 2), (3, 2)], "U0", full=[(2, 2)])
+        open_r2("t0", [(0, b) for b in ALL], "B1")
+        gather2(0, 0, 0, HALF)
+        gather2(0, 0, HALF, S)
+        r1_back(1)
+        open_r2("b1", [(2, 1), (3, 1)], "U3", full=[(2, 1)])
+        sig01 = sb([P, S], F32, "sig01")
+        gather2(0, 1, 0, HALF, sig01[:, :HALF])
+        gather2(0, 1, HALF, S, sig01[:, HALF:])
         gather1(2, 0)
         gather1(2, 1)
         add_first(2)
-        gather2(1, 0, HALF)
-        products(0, 0, HALF, 0, False)
-        add_second(2)
-        products(0, HALF, S, 0, True)
-        gather2(1, HALF, S)
-        tanh_and_back(0, 0, S)
-        open_sum(3, 0, P, "U0")
         gather1(3, 0)
-        gather2(2, 0, HALF)
-        gather1(3, 1)
-        products(1, 0, HALF, 0, False)
+        add_second(2)
+        product(0, 0, 0, HALF)
+        product(0, 0, HALF, S)
+        add_r2(0, 0, ALL)
         add_first(3)
-        gather2(2, HALF, S)
-        products(1, HALF, S, 0, True)
+        prod01 = sb([P, S], F32, "prod01")
+        product(0, 1, 0, HALF, prod01[:, :HALF])
+        product(0, 1, HALF, S, prod01[:, HALF:])
+        add_r2(0, 1, ALL)
+        for n in range(2):
+            gather2(1, n, 0, HALF)
+            gather2(1, n, HALF, S)
+        product(1, 0, 0, HALF)
+        prod10 = sb([P, HALF], F32, "prod10")
+        product(1, 0, HALF, S, prod10[:])
+        add_r2(1, 0, ALL)
+        gather1(3, 1, sig01[:])
+        tanh("t0")
+        backs = [bank(f"B{b}", f"back{b}") for b in range(4)]
+        back("t0")
+        tanh_window(2, "prod01")
+        product(1, 1, 0, HALF)
         add_second(3)
-        nc.scalar.activation(out=h_win[:], in_=u_win[3][:], func=ACT.Tanh)
-        products(2, 0, HALF, 0, True)
-        tanh_and_back(1, 0, S)
-        open_sum(3, P, 2 * P, "U1")
-        products(2, HALF, S, HALF, True)
-        gather_products(3, 0, P)
-        tanh_and_back(2, 0, HALF)
-        open_sum(3, 2 * P, 3 * P, "U2")
-        gather_products(3, P, 2 * P)
-        tanh_and_back(3, 0, P, 1.0)
-        tanh_and_back(2, HALF, S)
-        open_sum(3, 3 * P, S, "U3")
-        gather_products(3, 2 * P, 3 * P)
-        tanh_and_back(3, P, 2 * P, 1.0)
-        gather_products(3, 3 * P, S)
-        nc.vector.quantize_mx(out=w2_codes[:].bitcast(FP8X4), scales=w2_scales[:], in_=w2_b[:])
-        tanh_and_back(3, 2 * P, 3 * P, 1.0)
-        tanh_and_back(3, 3 * P, S, 1.0)
+        product(1, 1, HALF, S)
+        add_r2(1, 1, ALL)
+        for n in range(2):
+            gather2(2, n, 3 * P, S, prod10[:, blk(n)])
+        for b in range(2):
+            for n in range(2):
+                gather2(3, n, b * P, (b + 1) * P)
+        tanh("t1")
+        for n in range(2):
+            gather2(3, n, 2 * P, 3 * P)
+        for n in range(2):
+            gather_product(2, n, 0, P)
+            add_r2(2, n, [0])
+        for n in range(2):
+            product(3, n, 0, P)
+            add_r2(3, n, [0])
+        tanh("b0")
+        for n in range(2):
+            gather2(3, n, 3 * P, S)
+        for n in range(2):
+            gather_product(2, n, P, 2 * P)
+            add_r2(2, n, [1])
+        back("t1")
+        for n in range(2):
+            product(3, n, P, 2 * P)
+            add_r2(3, n, [1])
+        back("b0")
+        open_r2("b3", [(2, 3), (3, 3)], "U1")
+        tanh("b1")
+        for n in range(2):
+            gather_product(2, n, 2 * P, 3 * P)
+            add_r2(2, n, [2])
+        for n in range(2):
+            product(3, n, 2 * P, 3 * P)
+            add_r2(3, n, [2])
+        tanh("b2")
+        for t in (2, 3):
+            for n in range(2):
+                product(t, n, 3 * P, S)
+                add_r2(t, n, [3])
+        back("b1")
+        quantize_w2("sig3_1_256")
         gain(0)
+        back("b2")
+        tanh("b3")
         gain(1)
-        layer(0, ["U0"])
+        quantize_z(0)
+        back("b3")
+        layer(0, 0, 4, "U2")
+        store(0, 0, 4)
         gain(2)
-        layer(1, ["U1"])
-        layer(2, ["U2"])
+        quantize_z(1)
+        layer(1, 0, 4, "U3")
+        store(1, 0, 4)
         gain(3)
-        layer(3, ["U3", "B0"])
+        quantize_z(2)
+        quantize_z(3)
+        layer(2, 0, 4, "U0")
+        store(2, 0, 4)
+        layer(3, 0, 2, "U1")
+        layer(3, 2, 4, "B0")
+        store(3, 0, 2)
+        store(3, 2, 4, True)

@@ -19,7 +19,9 @@ ALU = mybir.AluOpType
 P = 128
 PACK = 4
 HALF = S // 2
-W1_VECTOR_M = 88
+W1_VECTOR_M = 60
+FIRST_PIECES = ((0, 256), (256, 512))
+FIRST_BANKS = ("U3", "B0")
 
 
 def tile_picked_mfield_none_p_kernel(
@@ -47,13 +49,14 @@ def tile_picked_mfield_none_p_kernel(
         w1_raw = sb([P, PACK, H], F32, "w1_raw")
         w2_raw = [sb([P, PACK, N // 2], F32, f"w2_raw{h}") for h in range(2)]
         gn_t = sb([P, PACK], F32, "gn_t")
-        cj = [[sb([P, S], F32, f"cj{n}_{t}") for n in range(2)] for t in range(PACK)]
+        cj_flat = [sb([P, 2 * S], F32, f"cj{t}") for t in range(PACK)]
+        cj = [c[:].rearrange("p (n j) -> p n j", n=2) for c in cj_flat]
         y_win = [sb([P, 2 * S], F32, f"y_win{t}") for t in range(PACK)]
         ident = sb([P, P], F32, "ident")
 
         nc.vector.memset(xs_win[:].bitcast(I32), 0)
         for q in range(4):
-            nc.sync.dma_start(
+            (nc.scalar if q < 2 else nc.sync).dma_start(
                 out=xs_rows[32 * q : 32 * q + 4, :].bitcast(I32),
                 in_=x_scales[0, 4 * q : 4 * q + 4, :].bitcast(I32),
             )
@@ -66,7 +69,7 @@ def tile_picked_mfield_none_p_kernel(
         cj_rows = [c.rearrange("(p t) j -> p t j", t=PACK) for c in (cj1, cj2)]
         for t in range(PACK):
             for n in range(2):
-                nc.sync.dma_start(out=cj[t][n][:], in_=cj_rows[n][:, t, :])
+                nc.sync.dma_start(out=cj[t][:, n, :], in_=cj_rows[n][:, t, :])
                 if t < 2 and n == 0:
                     nc.sync.dma_start(out=w2_raw[t][:], in_=w2_rows[:, :, t * HALF : (t + 1) * HALF])
         nc.sync.dma_start(out=gn_t[:], in_=gn.rearrange("(p t) o -> p (t o)", t=PACK))
@@ -93,10 +96,10 @@ def tile_picked_mfield_none_p_kernel(
         nc.vector.quantize_mx(out=w1_codes[:].bitcast(FP8X4), scales=w1_scales[:], in_=w1_b[:])
 
         xw_pick = sb([P, S], U32, "xw_pick")
-        for hf in range(2):
+        for lo, hi in FIRST_PIECES:
             nc.vector.tensor_copy(
-                out=xw_pick[:, hf * HALF : (hf + 1) * HALF],
-                in_=xw_win[:].bitcast(U32).indirect(offs_t[:, 16 * hf : 16 * hf + 16]),
+                out=xw_pick[:, lo:hi],
+                in_=xw_win[:].bitcast(U32).indirect(offs_t[:, lo // 16 : hi // 16]),
             )
 
         def field(t, lo, hi, tag):
@@ -113,8 +116,8 @@ def tile_picked_mfield_none_p_kernel(
             )
             nc.scalar.activation(out=y_win[t][:, lo:hi], in_=y_bank[:, : hi - lo], func=ACT.Copy, scale=0.5)
 
-        field(0, 0, HALF, "U3")
-        field(0, HALF, S, "B0")
+        for (lo, hi), tag in zip(FIRST_PIECES, FIRST_BANKS):
+            field(0, lo, hi, tag)
         for t in range(1, PACK):
             field(t, 0, S, f"B{t}")
 
@@ -131,15 +134,31 @@ def tile_picked_mfield_none_p_kernel(
             for b in range(4):
                 turn_into(r1_sum[t], b, y_win[t][:, blk(b)], start=(b == 0))
 
+        def open_r1_with_term(t, tag):
+            r1_sum[t] = bank(tag, f"r1_sum{t}")
+            for b in range(4):
+                turn_into(r1_sum[t], b, terms[t, 0][:, blk(b)], start=(b == 0))
+            for b in range(4):
+                turn_into(r1_sum[t], b, y_win[t][:, blk(b)])
+
         def gather1(t, n, into=None):
             terms[t, n] = sb([P, S], F32, f"term{t}_{n}")[:] if into is None else into
             nc.vector.tensor_tensor(
-                out=terms[t, n], in0=y_win[t][:].indirect(lists[n][:]), in1=cj[t][n][:], op=ALU.mult
+                out=terms[t, n], in0=y_win[t][:].indirect(lists[n][:]), in1=cj[t][:, n, :], op=ALU.mult
             )
 
         def add_r1(t, n):
             for b in range(4):
                 turn_into(r1_sum[t], b, terms[t, n][:, blk(b)], stop=(n == 1 and b == 3))
+
+        def first_half_wise(h, sum_tag, turn_tag):
+            cols = slice(h * HALF, (h + 1) * HALF)
+            nc.vector.tensor_tensor(
+                out=terms[0, 1][:, cols],
+                in0=y_win[0][:].indirect(lists[1][:, 16 * h : 16 * h + 16]),
+                in1=cj[0][:, 1, cols],
+                op=ALU.mult,
+            )
 
         def add_first(t, into=None):
             part[t] = sb([P, S], F32, f"part{t}")[:] if into is None else into
@@ -153,18 +172,26 @@ def tile_picked_mfield_none_p_kernel(
             part[t] = sb([P, S], F32, f"part{t}")[:] if into is None else into
             if into is None:
                 part[t] = part[t].rearrange("p (b j) -> p b j", j=P)
-            nc.scalar.copy(out=part[t], in_=r1_sum[t][:].rearrange("p (b j) -> p b j", j=P))
+            src = r1_sum[t][:].rearrange("p (b j) -> p b j", j=P)
+            if with_tanh:
+                nc.scalar.activation(out=part[t], in_=src, func=ACT.Tanh, scale=2.0)
+            else:
+                nc.scalar.copy(out=part[t], in_=src)
 
         def r1_turn(t, bank_tag):
             turned[t] = bank(bank_tag, f"turned{t}")
             for b in range(4):
                 nc.tensor.transpose(out=turned[t][:, blk(b)], in_=part[t][:, b, :], identity=ident[:])
 
-        def r1_back(t, tag=None):
+        def r1_back(t, halve=False, tag=None):
             win2[t] = keep.tile([P, S], F32, name=f"win2_{t}", tag=tag or f"win2_{t}", align_bytes=64)
-            nc.scalar.copy(out=win2[t][:], in_=turned[t][:])
+            if halve:
+                nc.scalar.activation(out=win2[t][:], in_=turned[t][:], func=ACT.Copy, scale=0.5)
+            else:
+                nc.scalar.copy(out=win2[t][:], in_=turned[t][:])
 
         where, left, whole, h_win, turned, prods, ths = {}, {}, set(), {}, {}, {}, {}
+        prods_flat = {}
 
         def open_r2(key, pieces, tag, full=()):
             sums[key] = bank(tag, f"sum_{key}")
@@ -186,26 +213,33 @@ def tile_picked_mfield_none_p_kernel(
             turn_into(sums[key], slot, src, stop=(left[key] == 0))
 
         def gather2(t, n, lo, hi, into=None):
-            sig[t, n, lo] = sb([P, hi - lo], F32, f"sig{t}_{n}_{lo}")[:] if into is None else into
+            if n == 0:
+                sig[t, lo] = (
+                    sb([P, 2 * (hi - lo)], F32, f"sig{t}_{lo}")[:].rearrange("p (n j) -> p n j", n=2) if into is None else into
+                )
             nc.scalar.activation(
-                out=sig[t, n, lo],
+                out=sig[t, lo][:, n, :],
                 in_=win2[t][:].indirect(lists[n][:, lo // 16 : hi // 16]),
                 func=ACT.Sigmoid,
                 scale=4.0,
             )
 
-        def product(t, n, lo, hi, into=None):
-            prod = sb([P, hi - lo], F32, f"prod{t}_{n}_{lo}")[:] if into is None else into
+        def product(t, lo, hi, into=None):
+            if into is None:
+                prods_flat[t, lo] = sb([P, 2 * (hi - lo)], F32, f"prod{t}_{lo}")[:]
+                into = prods_flat[t, lo].rearrange("p (n j) -> p n j", n=2)
+            prod = into
             nc.vector.scalar_tensor_tensor(
-                out=prod, in0=sig[t, n, lo], scalar=-0.5, in1=cj[t][n][:, lo:hi], op0=ALU.add, op1=ALU.mult
+                out=prod, in0=sig[t, lo], scalar=-0.5, in1=cj[t][:, :, lo:hi], op0=ALU.add, op1=ALU.mult
             )
-            for b in range(lo // P, hi // P):
-                prods[t, n, b] = prod[:, b * P - lo : (b + 1) * P - lo]
+            for n in range(2):
+                for b in range(lo // P, hi // P):
+                    prods[t, n, b] = prod[:, n, b * P - lo : (b + 1) * P - lo]
 
         def gather_product(t, n, lo, hi, into=None):
             prod = sb([P, hi - lo], F32, f"gprod{t}_{n}_{lo}")[:] if into is None else into
             nc.vector.tensor_tensor(
-                out=prod, in0=h_win.get(t, win2[t])[:].indirect(lists[n][:, lo // 16 : hi // 16]), in1=cj[t][n][:, lo:hi], op=ALU.mult
+                out=prod, in0=h_win.get(t, win2[t])[:].indirect(lists[n][:, lo // 16 : hi // 16]), in1=cj[t][:, n, lo:hi], op=ALU.mult
             )
             for b in range(lo // P, hi // P):
                 prods[t, n, b] = prod[:, b * P - lo : (b + 1) * P - lo]
@@ -233,9 +267,9 @@ def tile_picked_mfield_none_p_kernel(
         def gain(b, into=None):
             z_b[b] = sb([P, P * PACK], BF16, f"z{b}")[:] if into is None else into
             nc.vector.tensor_tensor(
-                out=z_b[b].rearrange("p (j t) -> p j t", t=PACK),
-                in0=backs[b][:].rearrange("p (t j) -> p j t", t=PACK),
-                in1=gn_t[:].unsqueeze(1).to_broadcast([P, P, PACK]),
+                out=z_b[b].rearrange("p (j e t) -> p j t e", e=2, t=PACK),
+                in0=backs[b][:].rearrange("p (t j e) -> p j t e", e=2, t=PACK),
+                in1=gn_t[:].unsqueeze(1).unsqueeze(3).to_broadcast([P, P // 2, PACK, 2]),
                 op=ALU.mult,
             )
 
@@ -287,108 +321,147 @@ def tile_picked_mfield_none_p_kernel(
             nc.vector.quantize_mx(out=w2_codes[:].bitcast(FP8X4), scales=w2_scales[:], in_=w2_b[:])
 
         ALL = range(4)
-        open_r1(0, "B0")
-        open_r1(1, "B1")
+        BLOCK_BANK = ("U2", "U0", "U3", "U1")
+
+
+        def pair(view):
+            return view.rearrange("p (n j) -> p n j", n=2)
+
+
+        def open_block(b):
+            open_r2(f"b{b}", [(t, b) for t in (2, 3)], BLOCK_BANK[b], full=[(2, 0), (2, 1), (2, 2)])
+
+
+        def add_both(t, blocks):
+            for b in blocks:
+                for n in (1, 0):
+                    add_r2(t, n, [b])
+
+
+        half_sum = [bank(tag, f"half_sum{h}") for h, tag in enumerate(("B0", "U0"))]
+        half_part = [sb([P, HALF], F32, f"half_part{h}") for h in range(2)]
+        half_turn = {}
+        win2[0] = sb([P, S], F32, "win2_0")
+
+
+        def half_add(h, src, start=False, stop=False):
+            for i in range(2):
+                turn_into(half_sum[h], i, src[:, blk(2 * h + i)], start=(start and i == 0), stop=(stop and i == 1))
+
+
+        def half_out(h):
+            nc.scalar.copy(out=half_part[h][:], in_=half_sum[h][:, :HALF])
+
+
+        def half_turn_back(h, tag):
+            half_turn[h] = bank(tag, f"half_turn{h}")
+            for i in range(2):
+                nc.tensor.transpose(out=half_turn[h][:, blk(i)], in_=half_part[h][:, blk(i)], identity=ident[:])
+
+
+        def half_back(h):
+            nc.scalar.copy(out=win2[0][:, h * HALF : (h + 1) * HALF], in_=half_turn[h][:, :HALF])
+
+
+        for h in range(2):
+            half_add(h, y_win[0], start=True)
         open_r2("t1", [(1, b) for b in ALL], "U1")
-        open_r2("b0", [(2, 0), (3, 0)], "U2", full=[(2, 0)])
         round_w2(0, 32)
         round_w2(32, 64)
         gather1(0, 0)
-        add_r1(0, 0)
-        gather1(0, 1)
-        add_r1(0, 1)
-        r1_out(0, False)
+        for h in range(2):
+            half_add(h, terms[0, 0])
+        terms[0, 1] = sb([P, S], F32, "term0_1")[:]
+        for h in range(2):
+            first_half_wise(h, None, None)
+            half_add(h, terms[0, 1], stop=True)
+        half_out(0)
+        half_out(1)
+        half_turn_back(0, "U3")
+        half_turn_back(1, "U2")
+        open_r1(1, "U0")
         round_w2(64, 96)
         round_w2(96, 128)
+        half_back(0)
+        half_back(1)
         gather1(1, 0)
         add_r1(1, 0)
-        r1_turn(0, "U0")
         gather1(1, 1)
         add_r1(1, 1)
-        r1_back(0)
+        open_block(0)
+        open_block(2)
+        for n in range(2):
+            gather2(0, n, 0, HALF)
         r1_out(1, False)
-        r1_turn(1, "U3")
-        open_r2("b2", [(2, 2), (3, 2)], "U0", full=[(2, 2)])
-        open_r2("t0", [(0, b) for b in ALL], "B1")
-        gather2(0, 0, 0, HALF)
-        gather2(0, 0, HALF, S)
+        r1_turn(1, "B3")
+        open_block(1)
+        sig0b = sb([P, S], F32, "sig0b")
+        for n in range(2):
+            gather2(0, n, HALF, S, pair(sig0b[:]))
         r1_back(1)
-        open_r2("b1", [(2, 1), (3, 1)], "U3", full=[(2, 1)])
-        sig01 = sb([P, S], F32, "sig01")
-        gather2(0, 1, 0, HALF, sig01[:, :HALF])
-        gather2(0, 1, HALF, S, sig01[:, HALF:])
+        open_r2("t0", [(0, b) for b in ALL], "B3")
         gather1(2, 0)
         gather1(2, 1)
         add_first(2)
         gather1(3, 0)
         add_second(2)
-        product(0, 0, 0, HALF)
-        product(0, 0, HALF, S)
-        add_r2(0, 0, ALL)
+        product(0, 0, HALF)
+        add_both(0, range(2))
         add_first(3)
-        prod01 = sb([P, S], F32, "prod01")
-        product(0, 1, 0, HALF, prod01[:, :HALF])
-        product(0, 1, HALF, S, prod01[:, HALF:])
-        add_r2(0, 1, ALL)
-        for n in range(2):
-            gather2(1, n, 0, HALF)
-            gather2(1, n, HALF, S)
-        product(1, 0, 0, HALF)
-        prod10 = sb([P, HALF], F32, "prod10")
-        product(1, 0, HALF, S, prod10[:])
-        add_r2(1, 0, ALL)
-        gather1(3, 1, sig01[:])
+        prod0b = sb([P, S], F32, "prod0b")
+        product(0, HALF, S, pair(prod0b[:]))
+        add_both(0, range(2, 4))
+        gather1(3, 1, sig[0, 0].rearrange("p n j -> p (n j)"))
+        add_second(3)
+        for lo in (0, HALF):
+            for n in range(2):
+                gather2(1, n, lo, lo + HALF)
+        tanh_window(2, "sig0b")
         tanh("t0")
         backs = [bank(f"B{b}", f"back{b}") for b in range(4)]
         back("t0")
-        tanh_window(2, "prod01")
-        product(1, 1, 0, HALF)
-        add_second(3)
-        product(1, 1, HALF, S)
-        add_r2(1, 1, ALL)
+        product(1, 0, HALF)
+        add_both(1, range(2))
+        prod1b = sb([P, S], F32, "prod1b")
+        product(1, HALF, S, pair(prod1b[:]))
+        add_both(1, range(2, 4))
         for n in range(2):
-            gather2(2, n, 3 * P, S, prod10[:, blk(n)])
+            gather2(2, n, 3 * P, S, pair(prod0b[:, P : 3 * P]))
         for b in range(2):
             for n in range(2):
                 gather2(3, n, b * P, (b + 1) * P)
         tanh("t1")
         for n in range(2):
-            gather2(3, n, 2 * P, 3 * P)
+            gather2(3, n, 2 * P, 3 * P, pair(prod1b[:, P : 3 * P]))
         for n in range(2):
-            gather_product(2, n, 0, P)
-            add_r2(2, n, [0])
-        for n in range(2):
-            product(3, n, 0, P)
-            add_r2(3, n, [0])
+            gather_product(2, n, 0, HALF)
+            add_r2(2, n, range(2))
+        product(3, 0, P)
+        add_both(3, [0])
+        back("t1")
         tanh("b0")
         for n in range(2):
-            gather2(3, n, 3 * P, S)
-        for n in range(2):
-            gather_product(2, n, P, 2 * P)
-            add_r2(2, n, [1])
-        back("t1")
-        for n in range(2):
-            product(3, n, P, 2 * P)
-            add_r2(3, n, [1])
-        back("b0")
-        open_r2("b3", [(2, 3), (3, 3)], "U1")
+            gather2(3, n, 3 * P, S, pair(prods_flat[3, 0]))
+        product(3, P, 2 * P)
+        add_both(3, [1])
         tanh("b1")
         for n in range(2):
-            gather_product(2, n, 2 * P, 3 * P)
+            gather_product(2, n, 2 * P, 3 * P, sig[3, 0][:, n, :])
             add_r2(2, n, [2])
-        for n in range(2):
-            product(3, n, 2 * P, 3 * P)
-            add_r2(3, n, [2])
-        tanh("b2")
-        for t in (2, 3):
-            for n in range(2):
-                product(t, n, 3 * P, S)
-                add_r2(t, n, [3])
+        back("b0")
+        product(3, 2 * P, 3 * P)
+        add_both(3, [2])
+        open_block(3)
+        product(2, 3 * P, S, pair(sig[1, HALF].rearrange("p n j -> p (n j)")[:, :HALF]))
+        add_both(2, [3])
         back("b1")
-        quantize_w2("sig3_1_256")
+        tanh("b2")
+        product(3, 3 * P, S)
+        add_both(3, [3])
+        quantize_w2("prod1b")
+        tanh("b3")
         gain(0)
         back("b2")
-        tanh("b3")
         gain(1)
         quantize_z(0)
         back("b3")
@@ -396,13 +469,13 @@ def tile_picked_mfield_none_p_kernel(
         store(0, 0, 4)
         gain(2)
         quantize_z(1)
-        layer(1, 0, 4, "U3")
+        layer(1, 0, 4, "U0")
         store(1, 0, 4)
         gain(3)
         quantize_z(2)
-        quantize_z(3)
-        layer(2, 0, 4, "U0")
+        layer(2, 0, 4, "U3")
         store(2, 0, 4)
+        quantize_z(3)
         layer(3, 0, 2, "U1")
         layer(3, 2, 4, "B0")
         store(3, 0, 2)

@@ -465,18 +465,18 @@ def tile_picked_mfield_none_p_kernel(
         gain(1)
         quantize_z(0)
         back("b3")
-        layer(0, 0, 4, "U2")
+        layer(0, 0, 4, "U1")
         store(0, 0, 4)
         gain(2)
         quantize_z(1)
-        layer(1, 0, 4, "U0")
+        layer(1, 0, 4, "U2")
         store(1, 0, 4)
         gain(3)
         quantize_z(2)
-        layer(2, 0, 4, "U3")
+        layer(2, 0, 4, "U0")
         store(2, 0, 4)
         quantize_z(3)
-        layer(3, 0, 2, "U1")
+        layer(3, 0, 2, "U3")
         layer(3, 2, 4, "B0")
         store(3, 0, 2)
         store(3, 2, 4, True)

@@ -329,7 +329,7 @@ def tile_picked_mfield_none_p_kernel(
 
 
         def open_block(b):
-            open_r2(f"b{b}", [(t, b) for t in (2, 3)], BLOCK_BANK[b], full=[(2, 0), (2, 1), (2, 2)])
+            open_r2(f"b{b}", [(t, b) for t in (2, 3)], BLOCK_BANK[b], full=[(2, b) for b in range(4)])
 
 
         def add_both(t, blocks):
@@ -425,8 +425,6 @@ def tile_picked_mfield_none_p_kernel(
         prod1b = sb([P, S], F32, "prod1b")
         product(1, HALF, S, pair(prod1b[:]))
         add_both(1, range(2, 4))
-        for n in range(2):
-            gather2(2, n, 3 * P, S, pair(prod0b[:, P : 3 * P]))
         for b in range(2):
             for n in range(2):
                 gather2(3, n, b * P, (b + 1) * P)
@@ -446,13 +444,12 @@ def tile_picked_mfield_none_p_kernel(
         add_both(3, [1])
         tanh("b1")
         for n in range(2):
-            gather_product(2, n, 2 * P, 3 * P, sig[3, 0][:, n, :])
+            gather_product(2, n, HALF, S, sig[1, HALF][:, n, :])
             add_r2(2, n, [2])
         back("b0")
         product(3, 2 * P, 3 * P)
         add_both(3, [2])
         open_block(3)
-        product(2, 3 * P, S, pair(sig[1, HALF].rearrange("p n j -> p (n j)")[:, :HALF]))
         add_both(2, [3])
         back("b1")
         tanh("b2")

@@ -43,7 +43,6 @@ def tile_picked_mfield_none_p_kernel(
         p2_t = sb([P, S // 16], U16, "p2_t")
         lists = (p1_t, p2_t)
 
-        xs_rows = sb([P, T], U8, "xs_rows")
         xs_win = sb([P, T], U8, "xs_win")
         xw_win = sb([P, T], I32, "xw_win")
         w1_raw = sb([P, PACK, H], F32, "w1_raw")
@@ -55,14 +54,18 @@ def tile_picked_mfield_none_p_kernel(
         ident = sb([P, P], F32, "ident")
 
         nc.vector.memset(xs_win[:].bitcast(I32), 0)
-        for q in range(4):
-            (nc.scalar if q < 2 else nc.sync).dma_start(
-                out=xs_rows[32 * q : 32 * q + 4, :].bitcast(I32),
-                in_=x_scales[0, 4 * q : 4 * q + 4, :].bitcast(I32),
-            )
         nc.sync.dma_start(out=offs_t[:], in_=offs)
-        nc.sync.dma_start(out=w1_raw[:], in_=w1.rearrange("(p j) c -> p j c", j=PACK))
+        w1_rows = w1.rearrange("(p j) c -> p j c", j=PACK)
+        nc.sync.dma_start(out=w1_raw[:, :1], in_=w1_rows[:, :1])
+        nc.sync.dma_start(out=xs_win[0:P:8, :].bitcast(I32), in_=x_scales[0].bitcast(I32))
+        nc.sync.dma_start(out=w1_raw[:, 1:], in_=w1_rows[:, 1:])
         nc.sync.dma_start(out=xw_win[:], in_=x_words[0].rearrange("p n r -> p (n r)").bitcast(I32))
+        xs_spread = sb([P, S], U8, "xs_spread")
+        nc.vector.tensor_copy(out=xs_spread[:], in_=xs_win[:].indirect(offs_t[:]))
+        xs_pick = sb([P, S], U8, "xs_pick")
+        nc.vector.tensor_copy(out=xs_pick[:].bitcast(I32), in_=xs_spread[:].bitcast(I32))
+        for i in range(1, 4):
+            nc.sync.dma_start(out=xs_pick[i:P:32, :].bitcast(I32), in_=xs_spread[8 * i : P : 32, :].bitcast(I32))
         nc.sync.dma_start(out=p1_t[:], in_=p1)
         nc.sync.dma_start(out=p2_t[:], in_=p2)
         w2_rows = w2.rearrange("(p j) c -> p j c", j=PACK)
@@ -80,11 +83,6 @@ def tile_picked_mfield_none_p_kernel(
         warm = sb([P, 1], F32, "warm")
         nc.scalar.activation(out=warm[:], in_=y_win[0][:, S : S + 1], func=ACT.Sigmoid)
 
-        for q in range(4):
-            rows = slice(32 * q, 32 * q + 4)
-            nc.vector.tensor_copy(out=xs_win[rows, :].bitcast(I32), in_=xs_rows[rows, :].bitcast(I32))
-        xs_pick = sb([P, S], U8, "xs_pick")
-        nc.vector.tensor_copy(out=xs_pick[:], in_=xs_win[:].indirect(offs_t[:]))
 
         w1_b = sb([P, PACK * H], BF16, "w1_b")
         w1_dst = w1_b[:].rearrange("p (t m j) -> p m j t", t=PACK, j=PACK)

@@ -19,7 +19,7 @@ ALU = mybir.AluOpType
 P = 128
 PACK = 4
 HALF = S // 2
-W1_VECTOR_M = 60
+W1_VECTOR_M = 84
 FIRST_PIECES = ((0, 256), (256, 512))
 FIRST_BANKS = ("U3", "B0")
 
@@ -54,9 +54,9 @@ def tile_picked_mfield_none_p_kernel(
         ident = sb([P, P], F32, "ident")
 
         nc.vector.memset(xs_win[:].bitcast(I32), 0)
-        nc.sync.dma_start(out=offs_t[:], in_=offs)
         w1_rows = w1.rearrange("(p j) c -> p j c", j=PACK)
         nc.sync.dma_start(out=w1_raw[:, :1], in_=w1_rows[:, :1])
+        nc.sync.dma_start(out=offs_t[:], in_=offs)
         nc.sync.dma_start(out=xs_win[0:P:8, :].bitcast(I32), in_=x_scales[0].bitcast(I32))
         nc.sync.dma_start(out=w1_raw[:, 1:], in_=w1_rows[:, 1:])
         nc.sync.dma_start(out=xw_win[:], in_=x_words[0].rearrange("p n r -> p (n r)").bitcast(I32))

@@ -20,6 +20,7 @@ P = 128
 PACK = 4
 HALF = S // 2
 W1_VECTOR_M = 84
+FIELD_SCALE = (0.5, 0.5, 1.0, 0.5)
 FIRST_PIECES = ((0, 256), (256, 512))
 FIRST_BANKS = ("U3", "B0")
 
@@ -112,7 +113,7 @@ def tile_picked_mfield_none_p_kernel(
                 start=True,
                 stop=True,
             )
-            nc.scalar.activation(out=y_win[t][:, lo:hi], in_=y_bank[:, : hi - lo], func=ACT.Copy, scale=0.5)
+            nc.scalar.activation(out=y_win[t][:, lo:hi], in_=y_bank[:, : hi - lo], func=ACT.Copy, scale=FIELD_SCALE[t])
 
         for (lo, hi), tag in zip(FIRST_PIECES, FIRST_BANKS):
             field(0, lo, hi, tag)
@@ -199,11 +200,10 @@ def tile_picked_mfield_none_p_kernel(
                 turn_into(sums[key], slot, y_win[t][:, blk(b)], start=(slot == 0))
                 if (t, b) in full:
                     whole.add((t, b))
-                    turn_into(sums[key], slot, y_win[t][:, blk(b)])
 
         def tanh_window(t, tag=None):
             h_win[t] = keep.tile([P, S], F32, name=f"h_win{t}", tag=tag or f"h_win{t}", align_bytes=64)
-            nc.scalar.activation(out=h_win[t][:], in_=win2[t][:], func=ACT.Tanh, scale=2.0)
+            nc.scalar.activation(out=h_win[t][:], in_=win2[t][:], func=ACT.Tanh, scale=1.0 / FIELD_SCALE[t])
 
         def add_term(t, b, src):
             key, slot = where[t, b]
@@ -257,10 +257,11 @@ def tile_picked_mfield_none_p_kernel(
                 nc.scalar.activation(out=th[:, cut:], in_=sums[key][:, cut:width], func=ACT.Tanh, scale=2.0)
             ths[key] = (th, pieces)
 
-        def back(key):
+        def back(key, blocks=range(4)):
             th, pieces = ths[key]
             for slot, t, b in pieces:
-                nc.tensor.transpose(out=backs[b][:, blk(t)], in_=th[:, blk(slot)], identity=ident[:])
+                if b in blocks:
+                    nc.tensor.transpose(out=backs[b][:, blk(t)], in_=th[:, blk(slot)], identity=ident[:])
 
         def gain(b, into=None):
             z_b[b] = sb([P, P * PACK], BF16, f"z{b}")[:] if into is None else into
@@ -363,7 +364,7 @@ def tile_picked_mfield_none_p_kernel(
 
         for h in range(2):
             half_add(h, y_win[0], start=True)
-        open_r2("t1", [(1, b) for b in ALL], "U1")
+        open_r2("t1", [(1, b) for b in ALL], "B2")
         round_w2(0, 32)
         round_w2(32, 64)
         gather1(0, 0)
@@ -386,18 +387,19 @@ def tile_picked_mfield_none_p_kernel(
         add_r1(1, 0)
         gather1(1, 1)
         add_r1(1, 1)
+        open_r2("t0", [(0, b) for b in ALL], "B3")
+        open_block(3)
         open_block(0)
         open_block(2)
         for n in range(2):
             gather2(0, n, 0, HALF)
         r1_out(1, False)
-        r1_turn(1, "B3")
+        r1_turn(1, "B1")
         open_block(1)
         sig0b = sb([P, S], F32, "sig0b")
         for n in range(2):
             gather2(0, n, HALF, S, pair(sig0b[:]))
         r1_back(1)
-        open_r2("t0", [(0, b) for b in ALL], "B3")
         gather1(2, 0)
         gather1(2, 1)
         add_first(2)
@@ -416,8 +418,8 @@ def tile_picked_mfield_none_p_kernel(
                 gather2(1, n, lo, lo + HALF)
         tanh_window(2, "sig0b")
         tanh("t0")
-        backs = [bank(f"B{b}", f"back{b}") for b in range(4)]
-        back("t0")
+        backs = {b: bank(f"B{b}", f"back{b}") for b in (0, 1, 3)}
+        back("t0", (0, 1, 3))
         product(1, 0, HALF)
         add_both(1, range(2))
         prod1b = sb([P, S], F32, "prod1b")
@@ -434,7 +436,9 @@ def tile_picked_mfield_none_p_kernel(
             add_r2(2, n, range(2))
         product(3, 0, P)
         add_both(3, [0])
+        backs[2] = bank("B2", "back2")
         back("t1")
+        back("t0", (2,))
         tanh("b0")
         for n in range(2):
             gather2(3, n, 3 * P, S, pair(prods_flat[3, 0]))
@@ -443,12 +447,10 @@ def tile_picked_mfield_none_p_kernel(
         tanh("b1")
         for n in range(2):
             gather_product(2, n, HALF, S, sig[1, HALF][:, n, :])
-            add_r2(2, n, [2])
+            add_r2(2, n, [2, 3])
         back("b0")
         product(3, 2 * P, 3 * P)
         add_both(3, [2])
-        open_block(3)
-        add_both(2, [3])
         back("b1")
         tanh("b2")
         product(3, 3 * P, S)

from contextlib import ExitStack

import concourse.mybir as mybir
from concourse.masks import make_identity

K, T, S, H, N = 512, 2048, 512, 512, 512
FLOPS = 2 * K * H * S + 2 * H * N * S

F32 = mybir.dt.float32
BF16 = mybir.dt.bfloat16
I32 = mybir.dt.int32
U32 = mybir.dt.uint32
U16 = mybir.dt.uint16
U8 = mybir.dt.uint8
FP8X4 = mybir.dt.float8_e4m3fn_x4
ACT = mybir.ActivationFunctionType
ALU = mybir.AluOpType

P = 128
PACK = 4
HALF = S // 2
W1_VECTOR_M = 84
FIELD_SCALE = (0.5, 0.5, 1.0, 0.5)
FIRST_PIECES = ((0, 256), (256, 512))
FIRST_BANKS = ("U3", "B0")


def tile_picked_mfield_none_p_kernel(
    tc, x_words, x_scales, w1, cj1, cj2, gn, w2, offs, p1, p2, out
):
    nc = tc.nc
    with ExitStack() as ctx:
        keep = ctx.enter_context(tc.tile_pool(name="keep", bufs=1))
        psum = ctx.enter_context(tc.psum_pool(name="psum", bufs=1))

        def sb(shape, dtype, name):
            return keep.tile(shape, dtype, name=name, align_bytes=64)

        def bank(tag, name):
            return psum.tile([P, 512], F32, name=name, tag=tag)

        offs_t = sb([P, S // 16], U16, "offs_t")
        p1_t = sb([P, S // 16], U16, "p1_t")
        p2_t = sb([P, S // 16], U16, "p2_t")
        lists = (p1_t, p2_t)

        xs_win = sb([P, T], U8, "xs_win")
        xw_win = sb([P, T], I32, "xw_win")
        w1_raw = sb([P, PACK, H], F32, "w1_raw")
        w2_raw = [sb([P, PACK, N // 2], F32, f"w2_raw{h}") for h in range(2)]
        gn_t = sb([P, PACK], F32, "gn_t")
        cj_flat = [sb([P, 2 * S], F32, f"cj{t}") for t in range(PACK)]
        cj = [c[:].rearrange("p (n j) -> p n j", n=2) for c in cj_flat]
        y_win = [sb([P, 2 * S], F32, f"y_win{t}") for t in range(PACK)]
        ident = sb([P, P], F32, "ident")

        nc.vector.memset(xs_win[:].bitcast(I32), 0)
        w1_rows = w1.rearrange("(p j) c -> p j c", j=PACK)
        nc.sync.dma_start(out=w1_raw[:, :1], in_=w1_rows[:, :1])
        nc.sync.dma_start(out=offs_t[:], in_=offs)
        nc.sync.dma_start(out=xs_win[0:P:8, :].bitcast(I32), in_=x_scales[0].bitcast(I32))
        nc.sync.dma_start(out=w1_raw[:, 1:], in_=w1_rows[:, 1:])
        nc.sync.dma_start(out=xw_win[:], in_=x_words[0].rearrange("p n r -> p (n r)").bitcast(I32))
        xs_spread = sb([P, S], U8, "xs_spread")
        nc.vector.tensor_copy(out=xs_spread[:], in_=xs_win[:].indirect(offs_t[:]))
        xs_pick = sb([P, S], U8, "xs_pick")
        nc.vector.tensor_copy(out=xs_pick[:].bitcast(I32), in_=xs_spread[:].bitcast(I32))
        for i in range(1, 4):
            nc.sync.dma_start(out=xs_pick[i:P:32, :].bitcast(I32), in_=xs_spread[8 * i : P : 32, :].bitcast(I32))
        nc.sync.dma_start(out=p1_t[:], in_=p1)
        nc.sync.dma_start(out=p2_t[:], in_=p2)
        w2_rows = w2.rearrange("(p j) c -> p j c", j=PACK)
        cj_rows = [c.rearrange("(p t) j -> p t j", t=PACK) for c in (cj1, cj2)]
        for t in range(PACK):
            for n in range(2):
                nc.sync.dma_start(out=cj[t][:, n, :], in_=cj_rows[n][:, t, :])
                if t < 2 and n == 0:
                    nc.sync.dma_start(out=w2_raw[t][:], in_=w2_rows[:, :, t * HALF : (t + 1) * HALF])
        nc.sync.dma_start(out=gn_t[:], in_=gn.rearrange("(p t) o -> p (t o)", t=PACK))

        for t in range(PACK):
            nc.vector.memset(y_win[t][:, S:], 0.0)
        make_identity(nc, ident[:])
        warm = sb([P, 1], F32, "warm")
        nc.scalar.activation(out=warm[:], in_=y_win[0][:, S : S + 1], func=ACT.Sigmoid)


        w1_b = sb([P, PACK * H], BF16, "w1_b")
        w1_dst = w1_b[:].rearrange("p (t m j) -> p m j t", t=PACK, j=PACK)
        w1_src = w1_raw[:].rearrange("p j (m t) -> p m j t", t=PACK)
        nc.vector.tensor_copy(out=w1_dst[:, :W1_VECTOR_M], in_=w1_src[:, :W1_VECTOR_M])
        nc.scalar.copy(out=w1_dst[:, W1_VECTOR_M:], in_=w1_src[:, W1_VECTOR_M:])
        w1_codes = sb([P, H], U32, "w1_codes")
        w1_scales = sb([P, H], U8, "w1_scales")
        nc.vector.quantize_mx(out=w1_codes[:].bitcast(FP8X4), scales=w1_scales[:], in_=w1_b[:])

        xw_pick = sb([P, S], U32, "xw_pick")
        for lo, hi in FIRST_PIECES:
            nc.vector.tensor_copy(
                out=xw_pick[:, lo:hi],
                in_=xw_win[:].bitcast(U32).indirect(offs_t[:, lo // 16 : hi // 16]),
            )

        def field(t, lo, hi, tag):
            cols = slice(t * P, (t + 1) * P)
            y_bank = bank(tag, f"y_bank{t}_{lo}")
            nc.tensor.matmul_mx(
                out=y_bank[:, : hi - lo],
                lhsT=w1_codes[:, cols].bitcast(FP8X4),
                lhsT_scale=w1_scales[:, cols],
                rhs=xw_pick[:, lo:hi].bitcast(FP8X4),
                rhs_scale=xs_pick[:, lo:hi],
                start=True,
                stop=True,
            )
            nc.scalar.activation(out=y_win[t][:, lo:hi], in_=y_bank[:, : hi - lo], func=ACT.Copy, scale=FIELD_SCALE[t])

        for (lo, hi), tag in zip(FIRST_PIECES, FIRST_BANKS):
            field(0, lo, hi, tag)
        for t in range(1, PACK):
            field(t, 0, S, f"B{t}")

        terms, part, r1_sum, sums, sig, z_b, win2 = {}, {}, {}, {}, {}, {}, {}

        def blk(b):
            return slice(b * P, (b + 1) * P)

        def turn_into(acc, slot, src, start=False, stop=False):
            nc.tensor.matmul(out=acc[:, blk(slot)], lhsT=src, rhs=ident[:], start=start, stop=stop, is_transpose=True)

        def open_r1(t, tag):
            r1_sum[t] = bank(tag, f"r1_sum{t}")
            for b in range(4):
                turn_into(r1_sum[t], b, y_win[t][:, blk(b)], start=(b == 0))

        def open_r1_with_term(t, tag):
            r1_sum[t] = bank(tag, f"r1_sum{t}")
            for b in range(4):
                turn_into(r1_sum[t], b, terms[t, 0][:, blk(b)], start=(b == 0))
            for b in range(4):
                turn_into(r1_sum[t], b, y_win[t][:, blk(b)])

        def gather1(t, n, into=None):
            terms[t, n] = sb([P, S], F32, f"term{t}_{n}")[:] if into is None else into
            nc.vector.tensor_tensor(
                out=terms[t, n], in0=y_win[t][:].indirect(lists[n][:]), in1=cj[t][:, n, :], op=ALU.mult
            )

        def add_r1(t, n):
            for b in range(4):
                turn_into(r1_sum[t], b, terms[t, n][:, blk(b)], stop=(n == 1 and b == 3))

        def first_half_wise(h, sum_tag, turn_tag):
            cols = slice(h * HALF, (h + 1) * HALF)
            nc.vector.tensor_tensor(
                out=terms[0, 1][:, cols],
                in0=y_win[0][:].indirect(lists[1][:, 16 * h : 16 * h + 16]),
                in1=cj[0][:, 1, cols],
                op=ALU.mult,
            )

        def add_first(t, into=None):
            part[t] = sb([P, S], F32, f"part{t}")[:] if into is None else into
            nc.vector.tensor_tensor(out=part[t], in0=y_win[t][:, :S], in1=terms[t, 0], op=ALU.add)

        def add_second(t, tag=None):
            win2[t] = keep.tile([P, S], F32, name=f"win2_{t}", tag=tag or f"win2_{t}", align_bytes=64)
            nc.vector.tensor_tensor(out=win2[t][:], in0=part[t], in1=terms[t, 1], op=ALU.add)

        def r1_out(t, with_tanh, into=None):
            part[t] = sb([P, S], F32, f"part{t}")[:] if into is None else into
            if into is None:
                part[t] = part[t].rearrange("p (b j) -> p b j", j=P)
            src = r1_sum[t][:].rearrange("p (b j) -> p b j", j=P)
            if with_tanh:
                nc.scalar.activation(out=part[t], in_=src, func=ACT.Tanh, scale=2.0)
            else:
                nc.scalar.copy(out=part[t], in_=src)

        def r1_turn(t, bank_tag):
            turned[t] = bank(bank_tag, f"turned{t}")
            for b in range(4):
                nc.tensor.transpose(out=turned[t][:, blk(b)], in_=part[t][:, b, :], identity=ident[:])

        def r1_back(t, halve=False, tag=None):
            win2[t] = keep.tile([P, S], F32, name=f"win2_{t}", tag=tag or f"win2_{t}", align_bytes=64)
            if halve:
                nc.scalar.activation(out=win2[t][:], in_=turned[t][:], func=ACT.Copy, scale=0.5)
            else:
                nc.scalar.copy(out=win2[t][:], in_=turned[t][:])

        where, left, whole, h_win, turned, prods, ths = {}, {}, set(), {}, {}, {}, {}
        prods_flat = {}

        def open_r2(key, pieces, tag, full=()):
            sums[key] = bank(tag, f"sum_{key}")
            left[key] = 2 * len(pieces)
            for slot, (t, b) in enumerate(pieces):
                where[t, b] = (key, slot)
                turn_into(sums[key], slot, y_win[t][:, blk(b)], start=(slot == 0))
                if (t, b) in full:
                    whole.add((t, b))

        def tanh_window(t, tag=None):
            h_win[t] = keep.tile([P, S], F32, name=f"h_win{t}", tag=tag or f"h_win{t}", align_bytes=64)
            nc.scalar.activation(out=h_win[t][:], in_=win2[t][:], func=ACT.Tanh, scale=1.0 / FIELD_SCALE[t])

        def add_term(t, b, src):
            key, slot = where[t, b]
            left[key] = left[key] - 1
            turn_into(sums[key], slot, src, stop=(left[key] == 0))

        def gather2(t, n, lo, hi, into=None):
            if n == 0:
                sig[t, lo] = (
                    sb([P, 2 * (hi - lo)], F32, f"sig{t}_{lo}")[:].rearrange("p (n j) -> p n j", n=2) if into is None else into
                )
            nc.scalar.activation(
                out=sig[t, lo][:, n, :],
                in_=win2[t][:].indirect(lists[n][:, lo // 16 : hi // 16]),
                func=ACT.Sigmoid,
                scale=4.0,
            )

        def product(t, lo, hi, into=None):
            if into is None:
                prods_flat[t, lo] = sb([P, 2 * (hi - lo)], F32, f"prod{t}_{lo}")[:]
                into = prods_flat[t, lo].rearrange("p (n j) -> p n j", n=2)
            prod = into
            nc.vector.scalar_tensor_tensor(
                out=prod, in0=sig[t, lo], scalar=-0.5, in1=cj[t][:, :, lo:hi], op0=ALU.add, op1=ALU.mult
            )
            for n in range(2):
                for b in range(lo // P, hi // P):
                    prods[t, n, b] = prod[:, n, b * P - lo : (b + 1) * P - lo]

        def gather_product(t, n, lo, hi, into=None):
            prod = sb([P, hi - lo], F32, f"gprod{t}_{n}_{lo}")[:] if into is None else into
            nc.vector.tensor_tensor(
                out=prod, in0=h_win.get(t, win2[t])[:].indirect(lists[n][:, lo // 16 : hi // 16]), in1=cj[t][:, n, lo:hi], op=ALU.mult
            )
            for b in range(lo // P, hi // P):
                prods[t, n, b] = prod[:, b * P - lo : (b + 1) * P - lo]

        def add_r2(t, n, blocks):
            for b in blocks:
                add_term(t, b, prods[t, n, b])

        def tanh(key, into=None):
            pieces = sorted([(slot, t, b) for (t, b), (k, slot) in where.items() if k == key])
            width = len(pieces) * P
            th = sb([P, width], F32, f"th_{key}")[:] if into is None else into
            cut = P * len([1 for slot, t, b in pieces if (t, b) in whole])
            if cut > 0:
                nc.scalar.activation(out=th[:, :cut], in_=sums[key][:, :cut], func=ACT.Tanh, scale=1.0)
            if cut < width:
                nc.scalar.activation(out=th[:, cut:], in_=sums[key][:, cut:width], func=ACT.Tanh, scale=2.0)
            ths[key] = (th, pieces)

        def back(key, blocks=range(4)):
            th, pieces = ths[key]
            for slot, t, b in pieces:
                if b in blocks:
                    nc.tensor.transpose(out=backs[b][:, blk(t)], in_=th[:, blk(slot)], identity=ident[:])

        def gain(b, into=None):
            z_b[b] = sb([P, P * PACK], BF16, f"z{b}")[:] if into is None else into
            nc.vector.tensor_tensor(
                out=z_b[b].rearrange("p (j e t) -> p j t e", e=2, t=PACK),
                in0=backs[b][:].rearrange("p (t j e) -> p j t e", e=2, t=PACK),
                in1=gn_t[:].unsqueeze(1).unsqueeze(3).to_broadcast([P, P // 2, PACK, 2]),
                op=ALU.mult,
            )

        w2_scales = sb([P, N], U8, "w2_scales")
        out_rows = out.rearrange("(mb m) j -> m mb j", m=P)

        z_q, o_banks = {}, {}

        def quantize_z(b):
            z_codes = sb([P, P], U32, f"z_codes{b}")
            z_scales = sb([P, P], U8, f"z_scales{b}")
            nc.vector.quantize_mx(out=z_codes[:].bitcast(FP8X4), scales=z_scales[:], in_=z_b[b])
            z_q[b] = (z_codes, z_scales)

        def layer(b, lo, hi, tag):
            o_banks[b, lo] = bank(tag, f"o_bank{b}_{lo}")
            for mb in range(lo, hi):
                nc.tensor.matmul_mx(
                    out=o_banks[b, lo][:, blk(mb - lo)],
                    lhsT=w2_q["codes"][:, blk(mb)].bitcast(FP8X4),
                    lhsT_scale=w2_scales[:, blk(mb)],
                    rhs=z_q[b][0][:].bitcast(FP8X4),
                    rhs_scale=z_q[b][1][:],
                    start=True,
                    stop=True,
                )

        def store(b, lo, hi, on_vector=False):
            o_sb = sb([P, hi - lo, P], F32, f"o_sb{b}_{lo}")
            src = o_banks[b, lo][:, : (hi - lo) * P]
            if on_vector:
                nc.vector.tensor_copy(out=o_sb[:].rearrange("p a j -> p (a j)"), in_=src)
            else:
                nc.scalar.copy(out=o_sb[:].rearrange("p a j -> p (a j)"), in_=src)
            nc.sync.dma_start(out=out_rows[:, lo:hi, blk(b)], in_=o_sb[:])

        w2_b = sb([P, PACK * N], BF16, "w2_b")
        w2_dst = w2_b[:].rearrange("p (c i j) -> p c j i", i=4, j=PACK)
        w2_src = [raw[:].rearrange("p j (c i) -> p c j i", i=4) for raw in w2_raw]

        def round_w2(lo, hi):
            nc.scalar.copy(out=w2_dst[:, lo:hi], in_=w2_src[lo // 64][:, lo % 64 : lo % 64 + hi - lo])

        w2_q = {}

        def quantize_w2(tag="w2_codes"):
            w2_codes = keep.tile([P, N], U32, name="w2_codes", tag=tag, align_bytes=64)
            w2_q["codes"] = w2_codes
            nc.vector.quantize_mx(out=w2_codes[:].bitcast(FP8X4), scales=w2_scales[:], in_=w2_b[:])

        ALL = range(4)
        BLOCK_BANK = ("U2", "U0", "U3", "U1")


        def pair(view):
            return view.rearrange("p (n j) -> p n j", n=2)


        def open_block(b):
            open_r2(f"b{b}", [(t, b) for t in (2, 3)], BLOCK_BANK[b], full=[(2, b) for b in range(4)])


        def add_both(t, blocks):
            for b in blocks:
                for n in (1, 0):
                    add_r2(t, n, [b])


        half_sum = [bank(tag, f"half_sum{h}") for h, tag in enumerate(("B0", "U0"))]
        half_part = [sb([P, HALF], F32, f"half_part{h}") for h in range(2)]
        half_turn = {}
        win2[0] = sb([P, S], F32, "win2_0")


        def half_add(h, src, start=False, stop=False):
            for i in range(2):
                turn_into(half_sum[h], i, src[:, blk(2 * h + i)], start=(start and i == 0), stop=(stop and i == 1))


        def half_out(h):
            nc.scalar.copy(out=half_part[h][:], in_=half_sum[h][:, :HALF])


        def half_turn_back(h, tag):
            half_turn[h] = bank(tag, f"half_turn{h}")
            for i in range(2):
                nc.tensor.transpose(out=half_turn[h][:, blk(i)], in_=half_part[h][:, blk(i)], identity=ident[:])


        def half_back(h):
            nc.scalar.copy(out=win2[0][:, h * HALF : (h + 1) * HALF], in_=half_turn[h][:, :HALF])


        for h in range(2):
            half_add(h, y_win[0], start=True)
        open_r2("t1", [(1, b) for b in ALL], "B2")
        round_w2(0, 32)
        round_w2(32, 64)
        gather1(0, 0)
        for h in range(2):
            half_add(h, terms[0, 0])
        terms[0, 1] = sb([P, S], F32, "term0_1")[:]
        for h in range(2):
            first_half_wise(h, None, None)
            half_add(h, terms[0, 1], stop=True)
        half_out(0)
        half_out(1)
        half_turn_back(0, "U3")
        half_turn_back(1, "U2")
        open_r1(1, "U0")
        round_w2(64, 96)
        round_w2(96, 128)
        half_back(0)
        half_back(1)
        gather1(1, 0)
        add_r1(1, 0)
        gather1(1, 1)
        add_r1(1, 1)
        open_r2("t0", [(0, b) for b in ALL], "B3")
        open_block(3)
        open_block(0)
        open_block(2)
        for n in range(2):
            gather2(0, n, 0, HALF)
        r1_out(1, False)
        r1_turn(1, "B1")
        open_block(1)
        sig0b = sb([P, S], F32, "sig0b")
        for n in range(2):
            gather2(0, n, HALF, S, pair(sig0b[:]))
        r1_back(1)
        gather1(2, 0)
        gather1(2, 1)
        add_first(2)
        gather1(3, 0)
        add_second(2)
        product(0, 0, HALF)
        add_both(0, range(2))
        add_first(3)
        prod0b = sb([P, S], F32, "prod0b")
        product(0, HALF, S, pair(prod0b[:]))
        add_both(0, range(2, 4))
        gather1(3, 1, sig[0, 0].rearrange("p n j -> p (n j)"))
        add_second(3)
        for lo in (0, HALF):
            for n in range(2):
                gather2(1, n, lo, lo + HALF)
        tanh_window(2, "sig0b")
        tanh("t0")
        backs = {b: bank(f"B{b}", f"back{b}") for b in (0, 1, 3)}
        back("t0", (0, 1, 3))
        product(1, 0, HALF)
        add_both(1, range(2))
        prod1b = sb([P, S], F32, "prod1b")
        product(1, HALF, S, pair(prod1b[:]))
        add_both(1, range(2, 4))
        for b in range(2):
            for n in range(2):
                gather2(3, n, b * P, (b + 1) * P)
        tanh("t1")
        for n in range(2):
            gather2(3, n, 2 * P, 3 * P, pair(prod1b[:, P : 3 * P]))
        for n in range(2):
            gather_product(2, n, 0, HALF)
            add_r2(2, n, range(2))
        product(3, 0, P)
        add_both(3, [0])
        backs[2] = bank("B2", "back2")
        back("t1")
        back("t0", (2,))
        tanh("b0")
        for n in range(2):
            gather2(3, n, 3 * P, S, pair(prods_flat[3, 0]))
        product(3, P, 2 * P)
        add_both(3, [1])
        tanh("b1")
        for n in range(2):
            gather_product(2, n, HALF, S, sig[1, HALF][:, n, :])
            add_r2(2, n, [2, 3])
        back("b0")
        product(3, 2 * P, 3 * P)
        add_both(3, [2])
        back("b1")
        tanh("b2")
        product(3, 3 * P, S)
        add_both(3, [3])
        quantize_w2("prod1b")
        tanh("b3")
        gain(0)
        back("b2")
        gain(1)
        quantize_z(0)
        back("b3")
        layer(0, 0, 4, "U1")
        store(0, 0, 4)
        gain(2)
        quantize_z(1)
        layer(1, 0, 4, "U2")
        store(1, 0, 4)
        gain(3)
        quantize_z(2)
        layer(2, 0, 4, "U0")
        store(2, 0, 4)
        quantize_z(3)
        layer(3, 0, 2, "U3")
        layer(3, 2, 4, "B0")
        store(3, 0, 2)
        store(3, 2, 4, True)
